import numpy as np
import ml_dtypes


def mxq(x, axis, fmt="e4m3"):
    dtype, down = {"e4m3": (ml_dtypes.float8_e4m3fn, 7), "e5m2": (ml_dtypes.float8_e5m2, 14)}[fmt]
    v = np.moveaxis(np.asarray(x, np.float32).astype(ml_dtypes.bfloat16).astype(np.float64), axis, -1)
    blocks = v.reshape(v.shape[:-1] + (-1, 32))
    amax = np.abs(blocks).max(-1, keepdims=True)
    byte = np.maximum(np.where(amax > 0, np.frexp(amax)[1] - 1 + 127, 0) - down, 1)
    scale = np.exp2(byte - 127.0)
    codes = (blocks / scale).astype(np.float32).astype(dtype).astype(np.float64)
    return np.moveaxis((codes * scale).reshape(v.shape), -1, axis)


WIDE = False


def mx_kscale(k):
    if not WIDE:
        return np.ones(k)
    levels = np.array([10, -10, 5, -5, 0])
    if k % 512:
        return np.exp2(np.random.permutation(np.resize(levels, k // 32))).repeat(32)
    a = np.empty((k // 512, 16))
    for p in range(k // 512):
        a[p, :8] = np.random.permutation(np.resize(levels, 8))
        for g in range(8):
            far = levels[np.abs(levels - a[p, g]) >= 10]
            a[p, g + 8] = far[np.random.randint(len(far))]
    return np.exp2(a.ravel()).repeat(32)


BF16 = ml_dtypes.bfloat16


def bf(x):
    return np.asarray(x, np.float32).astype(BF16)


def f64(x):
    return np.asarray(x).astype(np.float64)


B, N, E, D, A = 128, 64, 1024, 512, 256


def cosine_features(tau, omega, gc):
    angles = omega[None, None, :] * tau[:, :, None]
    return np.cos(angles) * gc[None, None, :]


def draw0():
    s, t = mx_kscale(E), mx_kscale(D)
    return {
        "psi": bf(np.random.standard_normal((B, D)) * t[None, :]),
        "tau": bf(np.random.uniform(0.0, 1.0, (B, N))),
        "omega": bf(np.random.uniform(-4.5, 4.5, E)),
        "gc": bf((1.0 + 0.1 * np.random.standard_normal(E)) * s),
        "wc": bf(np.random.standard_normal((E, D)) * 1.4 / np.sqrt(E) / s[:, None]),
        "bc": bf(np.random.standard_normal(D) * 0.3),
        "wq": bf(np.random.standard_normal((D, A)) * 1.5 / np.sqrt(D) / t[:, None]),
    }


def core(psi, tau, omega, gc, wc, bc, wq):
    psi, tau, omega, gc, wc, bc, wq = f64(psi), f64(tau), f64(omega), f64(gc), f64(wc), f64(bc), f64(wq)
    c = cosine_features(tau, omega, gc)
    phi = np.maximum((mxq(c, 2, "e4m3") @ mxq(wc, 0, "e4m3")) + bc[None, None, :], 0.0)
    m = psi[:, None, :] * phi
    return mxq(m, 2, "e4m3") @ mxq(wq, 0, "e4m3")


def e4m3fn_bytes(y):
    return np.clip(np.asarray(y, np.float64), -448.0, 448.0).astype(np.float32).astype(ml_dtypes.float8_e4m3fn).view(np.uint8)


def e4m3fn_values(b):
    return np.asarray(b, np.uint8).view(ml_dtypes.float8_e4m3fn).astype(np.float64)


def setup_inputs():
    d = draw0()
    x0 = np.asarray(d['wc']).astype(np.float64)
    s = (np.max(np.abs(x0), axis=(1,), keepdims=True) / 448.0).astype(np.float32)
    out = {}
    for k, v in d.items():
        if k == 'wc':
            out['wc_bytes'] = e4m3fn_bytes(x0 / s.astype(np.float64))
            out['wc_scale'] = s
        else:
            out[k] = v
    return out


def reference(psi, tau, omega, gc, wc_bytes, wc_scale, bc, wq):
    return core(psi, tau, omega, gc, e4m3fn_values(wc_bytes) * wc_scale.astype(np.float64), bc, wq)

@@ -1,0 +1,449 @@
+import math
+from contextlib import ExitStack
+
+import concourse.mybir as mybir
+from concourse.masks import make_identity
+
+B, N, E, D, A = 128, 64, 1024, 512, 256
+FLOPS = 2 * B * N * (E * D + D * A)
+
+F32 = mybir.dt.float32
+BF16 = mybir.dt.bfloat16
+I32 = mybir.dt.int32
+U32 = mybir.dt.uint32
+U8 = mybir.dt.uint8
+FP8 = mybir.dt.float8_e4m3fn
+FP8X4 = mybir.dt.float8_e4m3fn_x4
+ALU = mybir.AluOpType
+ACT = mybir.ActivationFunctionType
+
+P = 128
+PACK = 4
+PASSES = E // (P * PACK)
+TILE_N = 4
+TOK = TILE_N * B
+TILES = N // TILE_N
+RUN = 2
+TERMS = 20
+MID = 13
+LOW = 7
+ROWS = 64
+SERIES_N = N // 2
+GROUP_N = 8
+KS = PASSES * PACK
+
+
+def VEC(s):
+    return s in ()
+
+
+def tile_iqnlearnedcosinequantilehead_t_kernel(tc, psi, tau, omega, gc, wc_bytes, wc_scale, bc, wq, out):
+    nc = tc.nc
+    with ExitStack() as ctx:
+        keep = ctx.enter_context(tc.tile_pool(name="keep", bufs=1))
+        work = ctx.enter_context(tc.tile_pool(name="work", bufs=2))
+        psum = ctx.enter_context(tc.psum_pool(name="psum", bufs=1))
+        ctx.enter_context(tc.manual_schedule())
+
+        def kept(name, shape, dtype):
+            return keep.tile(shape, dtype, name=name, align_bytes=64)
+
+        def staged(name, tag, shape, dtype, bufs):
+            return work.tile(shape, dtype, name=name, tag=tag, bufs=bufs, align_bytes=64)
+
+        def bank(tag, shape, dtype):
+            return psum.tile(shape, dtype, name=tag, tag=tag, bufs={"tau": 1, "series": 2, "first": 3, "second": 2}[tag])
+
+        tau_sb = kept("tau_sb", [P, N], BF16)
+        omega_sb = kept("omega_sb", [P, PASSES, PACK], BF16)
+        gc_sb = kept("gc_sb", [P, PASSES, PACK], BF16)
+        wc_scale_sb = kept("wc_scale_sb", [P, PASSES, PACK], F32)
+        wc_raw = kept("wc_raw", [P, PASSES, PACK * D], U8)
+        bc_sb = kept("bc_sb", [P, PACK], BF16)
+        psi_sb = kept("psi_sb", [P, D], BF16)
+        wq_raw = kept("wq_raw", [P, PACK, A], BF16)
+        nc.sync.dma_start(out=tau_sb[:], in_=tau)
+        nc.scalar.dma_start(out=omega_sb[:], in_=omega.rearrange("(g p t) -> p g t", p=P, t=PACK))
+        nc.sync.dma_start(out=wc_scale_sb[:], in_=wc_scale.rearrange("(g p t) o -> p g (t o)", p=P, t=PACK))
+        nc.scalar.dma_start(out=gc_sb[:], in_=gc.rearrange("(g p t) -> p g t", p=P, t=PACK))
+        nc.sync.dma_start(out=wc_raw[:], in_=wc_bytes.rearrange("(g p t) d -> p g (t d)", p=P, t=PACK))
+        nc.sync.dma_start(out=psi_sb[:], in_=psi)
+        nc.sync.dma_start(out=bc_sb[:], in_=bc.rearrange("(p t) -> p t", t=PACK))
+        nc.sync.dma_start(out=wq_raw[:], in_=wq.rearrange("(p t) a -> p t a", t=PACK))
+
+        ident = kept("ident", [P, P], BF16)
+        make_identity(nc, ident[:])
+        counts = kept("counts", [P, TERMS - 1], F32)
+        nc.gpsimd.iota(counts[:], pattern=[[1, TERMS - 1]], base=1, channel_multiplier=0, allow_small_or_imprecise_dtypes=True)
+        zero = kept("zero", [P, 1], F32)
+        nc.vector.memset(zero[:], 0.0)
+        one = kept("one", [P, 1], F32)
+        nc.vector.memset(one[:], 1.0)
+        inv = kept("inv", [P, TERMS], F32)
+        nc.scalar.activation(out=inv[:, 0:1], in_=zero[:], func=ACT.Sin)
+        half_pi = kept("half_pi", [P, 1], F32)
+        nc.vector.tensor_scalar(out=half_pi[:], in0=one[:], scalar1=math.pi / 2, scalar2=None, op0=ALU.mult)
+        seeds = kept("seeds", [P, PASSES * PACK, TERMS], F32)
+        nc.vector.memset(seeds[:], 0.0)
+        powers = kept("powers", [P, SERIES_N, TERMS], F32)
+        nc.vector.memset(powers[:], 1.0)
+        basis = []
+        for j in range(2):
+            z = kept("basis%d" % j, [P, 2 * GROUP_N * B], BF16)
+            nc.vector.memset(z[:].bitcast(I32), 0)
+            basis.append(z)
+
+        neg_freq = kept("neg_freq", [P, PASSES * PACK], F32)
+        omega_flat = omega_sb[:].rearrange("p g t -> p (g t)")
+        nc.vector.scalar_tensor_tensor(out=neg_freq[:], in0=omega_flat, scalar=-1.0, in1=omega_flat, op0=ALU.mult, op1=ALU.min)
+
+        tiles = {}
+
+        def spread_tau(n0):
+            ps = bank("tau", [P, GROUP_N * B], BF16)
+            for j in range(GROUP_N):
+                nc.tensor.transpose(ps[:, j * B:(j + 1) * B], tau_sb[:, n0 + j:n0 + j + 1].to_broadcast([P, P]), ident[:])
+            tiles["tau", n0] = ps
+
+        def cosine(index):
+            n0, k = index // KS * GROUP_N, index % KS
+            g, t = divmod(k, PACK)
+            if t == 0:
+                tiles["cos", n0, g] = staged("cos", "cos", [P, PACK, GROUP_N * B], F32, 4)
+            nc.scalar.activation(out=tiles["cos", n0, g][:, t, :], in_=tiles["tau", n0][:], func=ACT.Sin,
+                                 scale=neg_freq[:, k:k + 1], bias=half_pi[:])
+            if k == KS - 1 and n0 + GROUP_N < SERIES_N:
+                spread_tau(n0 + GROUP_N)
+
+        def walk_planes(planes):
+            return planes.rearrange("p t (c i) -> p c t i", i=RUN)
+
+        def walk_words(flat):
+            return flat.rearrange("p (c i t) -> p c t i", i=RUN, t=PACK)
+
+        def features_tile(n0, g):
+            c = staged("c_%d_%d" % (n0, g), "c", [P, TOK * PACK], BF16, 8)
+            tiles["c", n0, g] = c
+            return c
+
+        def gain(n0, g):
+            c = features_tile(n0, g)
+            first = n0 % GROUP_N * B
+            planes = tiles["cos", n0 - n0 % GROUP_N, g][:, :, first:first + TOK]
+            gains = gc_sb[:, g, :].unsqueeze(1).unsqueeze(3).to_broadcast([P, TOK // RUN, PACK, RUN])
+            nc.vector.tensor_tensor(out=walk_words(c[:]), in0=walk_planes(planes), in1=gains, op=ALU.mult)
+
+        def series_matmuls(n0, g, half):
+            ps = bank("series", [P, TOK // 2, 2, 2], BF16)
+            first = (n0 - SERIES_N) * B + half * (TOK // 2)
+            z = basis[first // (GROUP_N * B) % 2]
+            first = first % (GROUP_N * B)
+            moving = z[:].rearrange("p (h x) -> p x h", h=2)[:, first:first + TOK // 2, :]
+            for u in range(2):
+                nc.tensor.matmul(ps[:, :, u, :], lhsT=coef[:, g * 2 + u, :], rhs=moving, start=True, stop=True)
+            tiles["series", n0, g, half] = ps
+
+        def series_out(n0, g, half):
+            c = features_tile(n0, g) if half == 0 else tiles["c", n0, g]
+            width = TOK * PACK // 2
+            nc.scalar.copy(out=c[:, half * width:(half + 1) * width], in_=tiles["series", n0, g, half][:].rearrange("p x u h -> p (x u h)"))
+
+        def quantise(name, source, width, bufs):
+            codes = staged(name + "_codes", name + "_codes", [P, width], U32, bufs)
+            scales = staged(name + "_scales", name + "_scales", [P, width], U8, bufs)
+            nc.vector.quantize_mx(out=codes[:].bitcast(FP8X4), scales=scales[:], in_=source)
+            return codes, scales
+
+        def quantise_c(n0, g):
+            tiles["cq", n0, g] = quantise("c", tiles["c", n0, g][:], TOK, 4)
+
+        def first_matmul(n0, t):
+            ps = bank("first", [P, TOK], F32)
+            cols = slice(t * P, (t + 1) * P)
+            for g in range(PASSES):
+                codes, scales = tiles["cq", n0, g]
+                nc.tensor.matmul_mx(out=ps[:], lhsT=wc_q[g][0][:, cols].bitcast(FP8X4), lhsT_scale=wc_q[g][1][:, cols],
+                                    rhs=codes[:].bitcast(FP8X4), rhs_scale=scales[:], start=(g == 0), stop=(g == PASSES - 1))
+            tiles["first", n0, t] = ps
+
+        def bias_relu(n0, t):
+            if t == 0:
+                tiles["phi", n0] = staged("phi", "phi", [P, PACK, TOK], F32, 3)
+            nc.scalar.activation(out=tiles["phi", n0][:, t, :], in_=tiles["first", n0, t][:], func=ACT.Relu, bias=bc_sb[:, t:t + 1])
+
+        def modulate(n0):
+            m = staged("m", "m", [P, TOK * PACK], BF16, 3)
+            nc.vector.tensor_tensor(out=walk_words(m[:]), in0=walk_planes(tiles["phi", n0][:]),
+                                    in1=psi_walk[:].rearrange("p n (c t i) -> p (n c) t i", t=PACK, i=RUN), op=ALU.mult)
+            tiles["m", n0] = m
+
+        def quantise_m(n0):
+            tiles["mq", n0] = quantise("m", tiles["m", n0][:], TOK, 3)
+
+        def second_matmul(n0, half):
+            ps = bank("second", [P, 2, A], F32)
+            codes, scales = tiles["mq", n0]
+            for j in range(2):
+                cols = slice((half * 2 + j) * B, (half * 2 + j + 1) * B)
+                nc.tensor.matmul_mx(out=ps[:, j, :], lhsT=codes[:, cols].bitcast(FP8X4), lhsT_scale=scales[:, cols],
+                                    rhs=wq_q[0][:].bitcast(FP8X4), rhs_scale=wq_q[1][:], start=True, stop=True)
+            tiles["second", n0, half] = ps
+
+        def store(n0, half, engine):
+            res = staged("res", "res", [P, 2, A], F32, 6)
+            if engine == "scalar":
+                nc.scalar.copy(out=res[:], in_=tiles["second", n0, half][:])
+            else:
+                nc.vector.tensor_copy(out=res[:], in_=tiles["second", n0, half][:])
+            nc.sync.dma_start(out=out[:, n0 + half * 2:n0 + half * 2 + 2, :], in_=res[:])
+
+        trig = kept("trig", [P, KS, 4], F32)
+        nc.scalar.activation(out=trig[:, :, 0], in_=neg_freq[:], func=ACT.Sin, scale=0.5, bias=half_pi[:])
+        nc.scalar.activation(out=trig[:, :, 1], in_=neg_freq[:], func=ACT.Sin, scale=0.5)
+        spread_tau(0)
+        sines = list(range(SERIES_N // GROUP_N * KS))
+
+        def next_sines(count):
+            for index in sines[:count]:
+                cosine(index)
+                sines.remove(index)
+
+        next_sines(5)
+
+        steps = kept("steps", [P, KS, TERMS], F32)
+        scaled = kept("scaled", [P, KS, TERMS], F32)
+        terms = kept("terms", [P, KS, TERMS], F32)
+        nc.vector.reciprocal(out=inv[:, 1:], in_=counts[:])
+        nc.vector.tensor_scalar(out=powers[:, :, 1], in0=tau_sb[:, SERIES_N:], scalar1=2.0, scalar2=-1.0, op0=ALU.mult, op1=ALU.add)
+        nc.vector.scalar_tensor_tensor(out=steps[:], in0=neg_freq[:].unsqueeze(2).to_broadcast([P, KS, TERMS]), scalar=-0.5,
+                                       in1=inv[:].unsqueeze(1).to_broadcast([P, KS, TERMS]), op0=ALU.mult, op1=ALU.mult)
+
+        def double_powers(top):
+            more = min(top, TERMS - 1 - top)
+            nc.vector.tensor_tensor(out=powers[:, :, top + 1:top + 1 + more], in0=powers[:, :, 1:1 + more],
+                                    in1=powers[:, :, top:top + 1].to_broadcast([P, SERIES_N, more]), op=ALU.mult)
+
+        double_powers(1)
+        nc.vector.tensor_copy(out=seeds[:, :, 0], in_=gc_sb[:].rearrange("p g t -> p (g t)"))
+        double_powers(2)
+        nc.vector.tensor_scalar(out=trig[:, :, 2:4], in0=trig[:, :, 0:2], scalar1=-1.0, scalar2=None, op0=ALU.mult)
+        double_powers(4)
+        nc.vector.tensor_tensor_scan(out=scaled[:].rearrange("p k j -> p (k j)"), data0=steps[:].rearrange("p k j -> p (k j)"),
+                                     data1=seeds[:].rearrange("p k j -> p (k j)"), initial=0.0, op0=ALU.mult, op1=ALU.add)
+        double_powers(8)
+        nc.vector.tensor_tensor(out=terms[:].rearrange("p k (a b) -> p k a b", b=4), in0=scaled[:].rearrange("p k (a b) -> p k a b", b=4),
+                                in1=trig[:].unsqueeze(2).to_broadcast([P, KS, TERMS // 4, 4]), op=ALU.mult)
+        double_powers(16)
+
+        r0 = slice(0, TERMS)
+        r1 = slice(r0.stop, r0.stop + MID)
+        r2 = slice(r1.stop, r1.stop + MID - 1)
+        r3 = slice(r2.stop, r2.stop + LOW)
+        r4 = slice(r3.stop, r3.stop + LOW - 1)
+        r5 = slice(r4.stop, r4.stop + LOW - 1)
+        assert r5.stop == ROWS
+        a_rows = kept("a_rows", [P, KS, ROWS], BF16)
+        a_rest = kept("a_rest", [P, KS, MID], F32)
+        b_rows = kept("b_rows", [P, SERIES_N, 2, ROWS], BF16)
+        b_rest = kept("b_rest", [P, SERIES_N, MID - 1], F32)
+        b_top = b_rows[:, :, 0, :]
+        nc.vector.tensor_copy(out=a_rows[:, :, r0], in_=terms[:])
+        nc.vector.tensor_copy(out=b_top[:, :, r0], in_=powers[:])
+        nc.vector.tensor_tensor(out=a_rest[:], in0=terms[:, :, 0:MID], in1=a_rows[:, :, 0:MID], op=ALU.subtract)
+        nc.vector.tensor_tensor(out=b_rest[:], in0=powers[:, :, 1:MID], in1=b_top[:, :, 1:MID], op=ALU.subtract)
+        nc.vector.tensor_copy(out=a_rows[:, :, r1], in_=a_rest[:])
+        nc.vector.tensor_copy(out=b_top[:, :, r2], in_=b_rest[:])
+        nc.vector.tensor_copy(out=a_rows[:, :, r2], in_=terms[:, :, 1:MID])
+        nc.vector.tensor_tensor(out=a_rows[:, :, r3], in0=a_rest[:, :, 0:LOW], in1=a_rows[:, :, r1.start:r1.start + LOW], op=ALU.subtract)
+        nc.vector.tensor_tensor(out=b_top[:, :, r5], in0=b_rest[:, :, 0:LOW - 1], in1=b_top[:, :, r2.start:r2.start + LOW - 1], op=ALU.subtract)
+        nc.vector.tensor_copy(out=a_rows[:, :, r4], in_=a_rest[:, :, 1:LOW])
+        nc.vector.tensor_copy(out=a_rows[:, :, r5], in_=terms[:, :, 1:LOW])
+        nc.vector.tensor_copy(out=b_top[:, :, r1], in_=powers[:, :, 0:MID])
+        nc.vector.tensor_copy(out=b_top[:, :, r3], in_=powers[:, :, 0:LOW])
+        nc.vector.tensor_copy(out=b_top[:, :, r4], in_=b_rest[:, :, 0:LOW - 1])
+
+        wides = []
+        for g in range(PASSES):
+            wide = kept("wc_wide%d" % g, [P, PACK, D], BF16)
+            for t in range(PACK):
+                nc.vector.tensor_scalar(out=wide[:, t, :], in0=wc_raw[:, g, t * D:(t + 1) * D].bitcast(FP8),
+                                        scalar1=wc_scale_sb[:, g, t:t + 1], scalar2=None, op0=ALU.mult)
+                if g == 0 and t == 0:
+                    nc.vector.tensor_copy(out=b_rows[:, :, 1, :], in_=b_top)
+            wides.append(wide)
+        grouped = []
+        for g in range(PASSES):
+            words = kept("wc_words%d" % g, [P, D * PACK], BF16)
+            nc.vector.tensor_copy(out=words[:].rearrange("p (t m j) -> p t m j", t=PACK, j=PACK),
+                                  in_=wides[g][:].rearrange("p j (m t) -> p t m j", t=PACK))
+            grouped.append(words)
+        wq_words = kept("wq_words", [P, A, PACK], BF16)
+        nc.vector.tensor_copy(out=wq_words[:], in_=wq_raw[:].rearrange("p j a -> p a j"))
+        wc_q = []
+        for g in range(PASSES):
+            wc_q.append(quantise("wc", grouped[g][:], D, PASSES))
+        wq_q = quantise("wq", wq_words[:].rearrange("p a j -> p (a j)"), A, 1)
+
+        coef = kept("coef", [P, KS // 2, P], BF16)
+        coef_ps = bank("second", [P, KS // 2, P], BF16)
+        for k in range(KS // 2):
+            nc.tensor.transpose(coef_ps[:, k, :], a_rows[:, 2 * k:2 * k + 2, :].rearrange("p h r -> p (h r)"), ident[:])
+        psi_ps = bank("second", [P, PACK, B], BF16)
+        for t in range(PACK):
+            nc.tensor.transpose(psi_ps[:, t, :], psi_sb[:, t::PACK], ident[:])
+
+        def turn_basis(j):
+            ps = bank("series", [P, GROUP_N * B], BF16)
+            for n in range(GROUP_N):
+                nc.tensor.transpose(ps[:, n * B:(n + 1) * B], b_rows[:, j * GROUP_N + n, :, :].rearrange("p h r -> p (h r)"), ident[:])
+            tiles["basis"] = ps
+
+        def basis_out(j, h, copy):
+            rows = slice(h * ROWS, (h + 1) * ROWS)
+            copy(out=basis[j % 2][rows, h * GROUP_N * B:(h + 1) * GROUP_N * B], in_=tiles["basis"][rows, :])
+
+        def unit(u):
+            return SERIES_N + u // PASSES * TILE_N, u % PASSES
+
+        def gain_unit(u):
+            if u < 4:
+                return u // 2 * TILE_N, u % 2
+            return u // 4 * GROUP_N + u % 2 * TILE_N, u // 2 % 2
+
+        turn_basis(0)
+        nc.scalar.copy(out=coef[:], in_=coef_ps[:])
+        psi_walk = kept("psi_walk", [P, TILE_N, B * PACK], BF16)
+        nc.scalar.copy(out=psi_walk[:, 0, :].rearrange("p (c t i) -> p c t i", t=PACK, i=RUN), in_=walk_planes(psi_ps[:]))
+        basis_out(0, 0, nc.scalar.copy)
+        basis_out(0, 1, nc.scalar.copy)
+        for u in range(3):
+            for half in range(2):
+                series_matmuls(*unit(u), half)
+            next_sines(2 if u else 1)
+            for half in range(2):
+                series_out(*unit(u), half)
+        turn_basis(1)
+        series_matmuls(*unit(3), 0)
+        next_sines(1)
+        basis_out(1, 0, nc.scalar.copy)
+        basis_out(1, 1, nc.scalar.copy)
+        series_matmuls(*unit(3), 1)
+        nc.vector.tensor_copy(out=psi_walk[:, 1:, :], in_=psi_walk[:, 0:1, :].to_broadcast([P, TILE_N - 1, B * PACK]))
+        gain(0, 0)
+        quantise_c(SERIES_N, 0)
+        quantise_c(SERIES_N, 1)
+        gain(0, 1)
+
+        order = []
+        for j in range(TILES // 2):
+            order.extend([SERIES_N + j * TILE_N, j * TILE_N])
+        order[-2:] = [order[-1], order[-2]]
+        UNITS = TILES
+        SINE_STEPS = 12
+        for s in range(TILES - 2):
+            now, soon = order[s], order[s + 1]
+            last = order[s - 1] if s > 0 else None
+            done = order[s - 2] if s > 1 else None
+            u = s + 3
+            share = -(-len(sines) // (SINE_STEPS - s)) if s < SINE_STEPS else 0
+            on_vector = done is not None and VEC(s)
+            turn = u + 2 < UNITS and (u + 2) % 4 == 0
+            first_matmul(now, 0)
+            if done is not None:
+                for half in range(2):
+                    second_matmul(done, half)
+            first_matmul(now, 1)
+            first_matmul(now, 2)
+            if u < UNITS:
+                series_out(*unit(u), 0)
+            next_sines(min(share, 1))
+            if u < UNITS:
+                series_out(*unit(u), 1)
+            if turn:
+                turn_basis((u + 2) // 4)
+            if u + 1 < UNITS:
+                series_matmuls(*unit(u + 1), 0)
+            if done is not None:
+                store(done, 0, "scalar")
+            bias_relu(now, 0)
+            first_matmul(now, 3)
+            if done is not None and not on_vector:
+                store(done, 1, "scalar")
+            bias_relu(now, 1)
+            bias_relu(now, 2)
+            bias_relu(now, 3)
+            next_sines(max(share - 1, 0))
+            gain(*gain_unit(s + 2))
+            if last is not None:
+                modulate(last)
+            if turn:
+                basis_out((u + 2) // 4, 0, nc.vector.tensor_copy)
+                basis_out((u + 2) // 4, 1, nc.vector.tensor_copy)
+            if u + 1 < UNITS:
+                series_matmuls(*unit(u + 1), 1)
+            if on_vector:
+                store(done, 1, "vector")
+            quantise_c(soon, 0)
+            quantise_c(soon, 1)
+            if last is not None:
+                quantise_m(last)
+
+        a, b, c, d = order[-4:]
+        for t in range(PACK - 1):
+            first_matmul(c, t)
+        for half in range(2):
+            second_matmul(a, half)
+        bias_relu(c, 0)
+        first_matmul(c, 3)
+        for t in range(1, PACK):
+            bias_relu(c, t)
+        store(a, 0, "scalar")
+        store(a, 1, "scalar")
+        quantise_c(d, 0)
+        modulate(b)
+        quantise_c(d, 1)
+        quantise_m(b)
+        phi = staged("phi", "phi", [P, PACK, TOK], F32, 3)
+        HALF = TOK // 2
+        for half in range(2):
+            cols = slice(half * HALF, (half + 1) * HALF)
+            for pair in range(2):
+                ps = bank("first", [P, 2, HALF], F32)
+                for j in range(2):
+                    t = 2 * pair + j
+                    for g in range(PASSES):
+                        codes, scales = tiles["cq", d, g]
+                        nc.tensor.matmul_mx(out=ps[:, j, :], lhsT=wc_q[g][0][:, t * P:(t + 1) * P].bitcast(FP8X4),
+                                            lhsT_scale=wc_q[g][1][:, t * P:(t + 1) * P], rhs=codes[:, cols].bitcast(FP8X4),
+                                            rhs_scale=scales[:, cols], start=(g == 0), stop=(g == PASSES - 1))
+                for j in range(2):
+                    t = 2 * pair + j
+                    nc.scalar.activation(out=phi[:, t, cols], in_=ps[:, j, :], func=ACT.Relu, bias=bc_sb[:, t:t + 1])
+            if half == 0:
+                second_matmul(b, 0)
+                second_matmul(b, 1)
+        store(b, 0, "scalar")
+        store(b, 1, "scalar")
+        modulate(c)
+        ms = []
+        for half in range(2):
+            m = staged("m", "m", [P, HALF * PACK], BF16, 3)
+            nc.vector.tensor_tensor(out=walk_words(m[:]), in0=walk_planes(phi[:, :, half * HALF:(half + 1) * HALF]),
+                                    in1=psi_walk[:, 0:2, :].rearrange("p n (c t i) -> p (n c) t i", t=PACK, i=RUN), op=ALU.mult)
+            ms.append(m)
+            if half == 0:
+                quantise_m(c)
+        second_matmul(c, 0)
+        second_matmul(c, 1)
+        store(c, 0, "scalar")
+        store(c, 1, "scalar")
+        for half in range(2):
+            codes, scales = quantise("m", ms[half][:], HALF, 3)
+            ps = bank("second", [P, 2, A], F32)
+            for j in range(2):
+                cols = slice(j * B, (j + 1) * B)
+                nc.tensor.matmul_mx(out=ps[:, j, :], lhsT=codes[:, cols].bitcast(FP8X4), lhsT_scale=scales[:, cols],
+                                    rhs=wq_q[0][:].bitcast(FP8X4), rhs_scale=wq_q[1][:], start=True, stop=True)
+            tiles["second", d, half] = ps
+        store(d, 0, "scalar")
+        store(d, 1, "vector")

@@ -31,10 +31,9 @@ ROWS = 64
 SERIES_N = N // 2
 GROUP_N = 8
 KS = PASSES * PACK
-
-
-def VEC(s):
-    return s in ()
+SHARE = 256
+LATE = 12
+EVERY = 2
 
 
 def tile_iqnlearnedcosinequantilehead_t_kernel(tc, psi, tau, omega, gc, wc_bytes, wc_scale, bc, wq, out):
@@ -52,7 +51,7 @@ def tile_iqnlearnedcosinequantilehead_t_kernel(tc, psi, tau, omega, gc, wc_bytes
             return work.tile(shape, dtype, name=name, tag=tag, bufs=bufs, align_bytes=64)
 
         def bank(tag, shape, dtype):
-            return psum.tile(shape, dtype, name=tag, tag=tag, bufs={"tau": 1, "series": 2, "first": 3, "second": 2}[tag])
+            return psum.tile(shape, dtype, name=tag, tag=tag, bufs={"tau": 1, "psi": 1, "series": 2, "first": 3, "second": 1}[tag])
 
         tau_sb = kept("tau_sb", [P, N], BF16)
         omega_sb = kept("omega_sb", [P, PASSES, PACK], BF16)
@@ -73,8 +72,6 @@ def tile_iqnlearnedcosinequantilehead_t_kernel(tc, psi, tau, omega, gc, wc_bytes
 
         ident = kept("ident", [P, P], BF16)
         make_identity(nc, ident[:])
-        counts = kept("counts", [P, TERMS - 1], F32)
-        nc.gpsimd.iota(counts[:], pattern=[[1, TERMS - 1]], base=1, channel_multiplier=0, allow_small_or_imprecise_dtypes=True)
         zero = kept("zero", [P, 1], F32)
         nc.vector.memset(zero[:], 0.0)
         one = kept("one", [P, 1], F32)
@@ -87,11 +84,15 @@ def tile_iqnlearnedcosinequantilehead_t_kernel(tc, psi, tau, omega, gc, wc_bytes
         nc.vector.memset(seeds[:], 0.0)
         powers = kept("powers", [P, SERIES_N, TERMS], F32)
         nc.vector.memset(powers[:], 1.0)
+        counts = kept("counts", [P, TERMS - 1], F32)
+        ones = powers[:, 0, 1:]
+        nc.vector.tensor_tensor_scan(out=counts[:], data0=ones, data1=ones, initial=0.0, op0=ALU.mult, op1=ALU.add)
         basis = []
         for j in range(2):
             z = kept("basis%d" % j, [P, 2 * GROUP_N * B], BF16)
-            nc.vector.memset(z[:].bitcast(I32), 0)
             basis.append(z)
+        nc.vector.memset(basis[0][:].bitcast(I32), 0)
+        nc.vector.reciprocal(out=inv[:, 1:], in_=counts[:])
 
         neg_freq = kept("neg_freq", [P, PASSES * PACK], F32)
         omega_flat = omega_sb[:].rearrange("p g t -> p (g t)")
@@ -121,17 +122,26 @@ def tile_iqnlearnedcosinequantilehead_t_kernel(tc, psi, tau, omega, gc, wc_bytes
         def walk_words(flat):
             return flat.rearrange("p (c i t) -> p c t i", i=RUN, t=PACK)
 
-        def features_tile(n0, g):
-            c = staged("c_%d_%d" % (n0, g), "c", [P, TOK * PACK], BF16, 8)
+        def features_tile(n0, g, tag="c", bufs=5):
+            c = staged("c_%d_%d" % (n0, g), tag, [P, TOK * PACK], BF16, bufs)
             tiles["c", n0, g] = c
             return c
 
-        def gain(n0, g):
-            c = features_tile(n0, g)
-            first = n0 % GROUP_N * B
-            planes = tiles["cos", n0 - n0 % GROUP_N, g][:, :, first:first + TOK]
-            gains = gc_sb[:, g, :].unsqueeze(1).unsqueeze(3).to_broadcast([P, TOK // RUN, PACK, RUN])
-            nc.vector.tensor_tensor(out=walk_words(c[:]), in0=walk_planes(planes), in1=gains, op=ALU.mult)
+        def cos_planes(n0, g, first, count):
+            first = first + n0 % GROUP_N * B
+            return tiles["cos", n0 - n0 % GROUP_N, g][:, :, first:first + count]
+
+        def gain(n0, g, first):
+            count = TOK - first
+            gains = gc_sb[:, g, :].unsqueeze(1).unsqueeze(3).to_broadcast([P, count // RUN, PACK, RUN])
+            nc.vector.tensor_tensor(out=walk_words(tiles["c", n0, g][:, first * PACK:]), in0=walk_planes(cos_planes(n0, g, first, count)),
+                                    in1=gains, op=ALU.mult)
+
+        def gain_on_gpsimd(n0, g, count):
+            c = features_tile(n0, g, "c_shared", 1)
+            nc.gpsimd.tensor_tensor(out=c[:, :count * PACK].rearrange("p (x t) -> p x t", t=PACK),
+                                    in0=cos_planes(n0, g, 0, count).rearrange("p t x -> p x t"),
+                                    in1=gc_sb[:, g, :].unsqueeze(1).to_broadcast([P, count, PACK]), op=ALU.mult)
 
         def series_matmuls(n0, g, half):
             ps = bank("series", [P, TOK // 2, 2, 2], BF16)
@@ -143,10 +153,10 @@ def tile_iqnlearnedcosinequantilehead_t_kernel(tc, psi, tau, omega, gc, wc_bytes
                 nc.tensor.matmul(ps[:, :, u, :], lhsT=coef[:, g * 2 + u, :], rhs=moving, start=True, stop=True)
             tiles["series", n0, g, half] = ps
 
-        def series_out(n0, g, half):
+        def series_out(n0, g, half, copy):
             c = features_tile(n0, g) if half == 0 else tiles["c", n0, g]
             width = TOK * PACK // 2
-            nc.scalar.copy(out=c[:, half * width:(half + 1) * width], in_=tiles["series", n0, g, half][:].rearrange("p x u h -> p (x u h)"))
+            copy(out=c[:, half * width:(half + 1) * width], in_=tiles["series", n0, g, half][:].rearrange("p x u h -> p (x u h)"))
 
         def quantise(name, source, width, bufs):
             codes = staged(name + "_codes", name + "_codes", [P, width], U32, bufs)
@@ -155,7 +165,7 @@ def tile_iqnlearnedcosinequantilehead_t_kernel(tc, psi, tau, omega, gc, wc_bytes
             return codes, scales
 
         def quantise_c(n0, g):
-            tiles["cq", n0, g] = quantise("c", tiles["c", n0, g][:], TOK, 4)
+            tiles["cq", n0, g] = quantise("c", tiles["c", n0, g][:], TOK, 9)
 
         def first_matmul(n0, t):
             ps = bank("first", [P, TOK], F32)
@@ -171,17 +181,21 @@ def tile_iqnlearnedcosinequantilehead_t_kernel(tc, psi, tau, omega, gc, wc_bytes
                 tiles["phi", n0] = staged("phi", "phi", [P, PACK, TOK], F32, 3)
             nc.scalar.activation(out=tiles["phi", n0][:, t, :], in_=tiles["first", n0, t][:], func=ACT.Relu, bias=bc_sb[:, t:t + 1])
 
+        def times_psi(words, planes, count):
+            nc.vector.tensor_tensor(out=words.rearrange("p (n c i t) -> p n c t i", n=count, i=RUN, t=PACK),
+                                    in0=planes.rearrange("p t (n c i) -> p n c t i", n=count, i=RUN),
+                                    in1=psi_ps[:].unsqueeze(1).to_broadcast([P, count, B // RUN, PACK, RUN]), op=ALU.mult)
+
         def modulate(n0):
             m = staged("m", "m", [P, TOK * PACK], BF16, 3)
-            nc.vector.tensor_tensor(out=walk_words(m[:]), in0=walk_planes(tiles["phi", n0][:]),
-                                    in1=psi_walk[:].rearrange("p n (c t i) -> p (n c) t i", t=PACK, i=RUN), op=ALU.mult)
+            times_psi(m[:], tiles["phi", n0][:], TILE_N)
             tiles["m", n0] = m
 
         def quantise_m(n0):
             tiles["mq", n0] = quantise("m", tiles["m", n0][:], TOK, 3)
 
-        def second_matmul(n0, half):
-            ps = bank("second", [P, 2, A], F32)
+        def second_matmul(n0, half, tag="second"):
+            ps = bank(tag, [P, 2, A], F32)
             codes, scales = tiles["mq", n0]
             for j in range(2):
                 cols = slice((half * 2 + j) * B, (half * 2 + j + 1) * B)
@@ -200,7 +214,11 @@ def tile_iqnlearnedcosinequantilehead_t_kernel(tc, psi, tau, omega, gc, wc_bytes
         trig = kept("trig", [P, KS, 4], F32)
         nc.scalar.activation(out=trig[:, :, 0], in_=neg_freq[:], func=ACT.Sin, scale=0.5, bias=half_pi[:])
         nc.scalar.activation(out=trig[:, :, 1], in_=neg_freq[:], func=ACT.Sin, scale=0.5)
+        nc.scalar.copy(out=basis[1][:], in_=basis[0][:])
         spread_tau(0)
+        psi_ps = bank("psi", [P, B // RUN, PACK, RUN], BF16)
+        for t in range(PACK):
+            nc.tensor.transpose(psi_ps[:, :, t, :], psi_sb[:, t::PACK], ident[:])
         sines = list(range(SERIES_N // GROUP_N * KS))
 
         def next_sines(count):
@@ -208,12 +226,11 @@ def tile_iqnlearnedcosinequantilehead_t_kernel(tc, psi, tau, omega, gc, wc_bytes
                 cosine(index)
                 sines.remove(index)
 
-        next_sines(5)
+        next_sines(6)
 
         steps = kept("steps", [P, KS, TERMS], F32)
         scaled = kept("scaled", [P, KS, TERMS], F32)
         terms = kept("terms", [P, KS, TERMS], F32)
-        nc.vector.reciprocal(out=inv[:, 1:], in_=counts[:])
         nc.vector.tensor_scalar(out=powers[:, :, 1], in0=tau_sb[:, SERIES_N:], scalar1=2.0, scalar2=-1.0, op0=ALU.mult, op1=ALU.add)
         nc.vector.scalar_tensor_tensor(out=steps[:], in0=neg_freq[:].unsqueeze(2).to_broadcast([P, KS, TERMS]), scalar=-0.5,
                                        in1=inv[:].unsqueeze(1).to_broadcast([P, KS, TERMS]), op0=ALU.mult, op1=ALU.mult)
@@ -288,9 +305,6 @@ def tile_iqnlearnedcosinequantilehead_t_kernel(tc, psi, tau, omega, gc, wc_bytes
         coef_ps = bank("second", [P, KS // 2, P], BF16)
         for k in range(KS // 2):
             nc.tensor.transpose(coef_ps[:, k, :], a_rows[:, 2 * k:2 * k + 2, :].rearrange("p h r -> p (h r)"), ident[:])
-        psi_ps = bank("second", [P, PACK, B], BF16)
-        for t in range(PACK):
-            nc.tensor.transpose(psi_ps[:, t, :], psi_sb[:, t::PACK], ident[:])
 
         def turn_basis(j):
             ps = bank("series", [P, GROUP_N * B], BF16)
@@ -312,27 +326,24 @@ def tile_iqnlearnedcosinequantilehead_t_kernel(tc, psi, tau, omega, gc, wc_bytes
 
         turn_basis(0)
         nc.scalar.copy(out=coef[:], in_=coef_ps[:])
-        psi_walk = kept("psi_walk", [P, TILE_N, B * PACK], BF16)
-        nc.scalar.copy(out=psi_walk[:, 0, :].rearrange("p (c t i) -> p c t i", t=PACK, i=RUN), in_=walk_planes(psi_ps[:]))
         basis_out(0, 0, nc.scalar.copy)
         basis_out(0, 1, nc.scalar.copy)
         for u in range(3):
             for half in range(2):
                 series_matmuls(*unit(u), half)
-            next_sines(2 if u else 1)
+            next_sines(1)
             for half in range(2):
-                series_out(*unit(u), half)
-        turn_basis(1)
-        series_matmuls(*unit(3), 0)
-        next_sines(1)
-        basis_out(1, 0, nc.scalar.copy)
-        basis_out(1, 1, nc.scalar.copy)
-        series_matmuls(*unit(3), 1)
-        nc.vector.tensor_copy(out=psi_walk[:, 1:, :], in_=psi_walk[:, 0:1, :].to_broadcast([P, TILE_N - 1, B * PACK]))
-        gain(0, 0)
+                series_out(*unit(u), half, nc.scalar.copy)
+        for half in range(2):
+            series_matmuls(*unit(3), half)
         quantise_c(SERIES_N, 0)
+        features_tile(0, 0)
+        gain(0, 0, 0)
         quantise_c(SERIES_N, 1)
-        gain(0, 1)
+        features_tile(0, 1, "c_shared", 1)
+        gain(0, 1, 0)
+        quantise_c(0, 0)
+        quantise_c(0, 1)
 
         order = []
         for j in range(TILES // 2):
@@ -341,67 +352,62 @@ def tile_iqnlearnedcosinequantilehead_t_kernel(tc, psi, tau, omega, gc, wc_bytes
         UNITS = TILES
         SINE_STEPS = 12
         for s in range(TILES - 2):
-            now, soon = order[s], order[s + 1]
+            now = order[s]
             last = order[s - 1] if s > 0 else None
             done = order[s - 2] if s > 1 else None
             u = s + 3
             share = -(-len(sines) // (SINE_STEPS - s)) if s < SINE_STEPS else 0
-            on_vector = done is not None and VEC(s)
-            turn = u + 2 < UNITS and (u + 2) % 4 == 0
-            first_matmul(now, 0)
+            turn = u + 1 < UNITS and (u + 1) % 4 == 0
+            gain_on_gpsimd(*gain_unit(s + 2), SHARE)
             if done is not None:
-                for half in range(2):
-                    second_matmul(done, half)
-            first_matmul(now, 1)
-            first_matmul(now, 2)
+                second_matmul(done, 0)
+            for t in range(PACK - 1):
+                first_matmul(now, t)
             if u < UNITS:
-                series_out(*unit(u), 0)
-            next_sines(min(share, 1))
-            if u < UNITS:
-                series_out(*unit(u), 1)
-            if turn:
-                turn_basis((u + 2) // 4)
-            if u + 1 < UNITS:
-                series_matmuls(*unit(u + 1), 0)
+                series_out(*unit(u), 0, nc.vector.tensor_copy if 0 < s < LATE and s % EVERY == 0 else nc.scalar.copy)
+                series_out(*unit(u), 1, nc.vector.tensor_copy if 0 < s < LATE else nc.scalar.copy)
+            if last is not None:
+                modulate(last)
             if done is not None:
                 store(done, 0, "scalar")
+                second_matmul(done, 1)
+            if turn:
+                turn_basis((u + 1) // 4)
+            elif u + 1 < UNITS:
+                series_matmuls(*unit(u + 1), 0)
+                series_matmuls(*unit(u + 1), 1)
+            next_sines(min(share, 1))
             bias_relu(now, 0)
             first_matmul(now, 3)
-            if done is not None and not on_vector:
-                store(done, 1, "scalar")
+            if turn:
+                basis_out((u + 1) // 4, 0, nc.scalar.copy)
+                basis_out((u + 1) // 4, 1, nc.scalar.copy)
+                series_matmuls(*unit(u + 1), 0)
+                series_matmuls(*unit(u + 1), 1)
             bias_relu(now, 1)
+            if done is not None:
+                store(done, 1, "scalar")
             bias_relu(now, 2)
             bias_relu(now, 3)
             next_sines(max(share - 1, 0))
-            gain(*gain_unit(s + 2))
-            if last is not None:
-                modulate(last)
-            if turn:
-                basis_out((u + 2) // 4, 0, nc.vector.tensor_copy)
-                basis_out((u + 2) // 4, 1, nc.vector.tensor_copy)
-            if u + 1 < UNITS:
-                series_matmuls(*unit(u + 1), 1)
-            if on_vector:
-                store(done, 1, "vector")
-            quantise_c(soon, 0)
-            quantise_c(soon, 1)
+            gain(*gain_unit(s + 2), SHARE)
             if last is not None:
                 quantise_m(last)
+            quantise_c(*unit(s + 2))
+            quantise_c(*gain_unit(s + 2))
 
         a, b, c, d = order[-4:]
+        second_matmul(a, 0)
+        store(a, 0, "scalar")
         for t in range(PACK - 1):
             first_matmul(c, t)
-        for half in range(2):
-            second_matmul(a, half)
+        second_matmul(a, 1)
         bias_relu(c, 0)
         first_matmul(c, 3)
         for t in range(1, PACK):
             bias_relu(c, t)
-        store(a, 0, "scalar")
         store(a, 1, "scalar")
-        quantise_c(d, 0)
         modulate(b)
-        quantise_c(d, 1)
         quantise_m(b)
         phi = staged("phi", "phi", [P, PACK, TOK], F32, 3)
         HALF = TOK // 2
@@ -419,27 +425,25 @@ def tile_iqnlearnedcosinequantilehead_t_kernel(tc, psi, tau, omega, gc, wc_bytes
                 for j in range(2):
                     t = 2 * pair + j
                     nc.scalar.activation(out=phi[:, t, cols], in_=ps[:, j, :], func=ACT.Relu, bias=bc_sb[:, t:t + 1])
-            if half == 0:
-                second_matmul(b, 0)
-                second_matmul(b, 1)
+        modulate(c)
+        second_matmul(b, 0, "series")
+        second_matmul(b, 1, "series")
         store(b, 0, "scalar")
         store(b, 1, "scalar")
-        modulate(c)
         ms = []
         for half in range(2):
             m = staged("m", "m", [P, HALF * PACK], BF16, 3)
-            nc.vector.tensor_tensor(out=walk_words(m[:]), in0=walk_planes(phi[:, :, half * HALF:(half + 1) * HALF]),
-                                    in1=psi_walk[:, 0:2, :].rearrange("p n (c t i) -> p (n c) t i", t=PACK, i=RUN), op=ALU.mult)
+            times_psi(m[:], phi[:, :, half * HALF:(half + 1) * HALF], 2)
             ms.append(m)
             if half == 0:
                 quantise_m(c)
-        second_matmul(c, 0)
-        second_matmul(c, 1)
+        second_matmul(c, 0, "series")
+        second_matmul(c, 1, "series")
         store(c, 0, "scalar")
         store(c, 1, "scalar")
         for half in range(2):
             codes, scales = quantise("m", ms[half][:], HALF, 3)
-            ps = bank("second", [P, 2, A], F32)
+            ps = bank("first", [P, 2, A], F32)
             for j in range(2):
                 cols = slice(j * B, (j + 1) * B)
                 nc.tensor.matmul_mx(out=ps[:, j, :], lhsT=codes[:, cols].bitcast(FP8X4), lhsT_scale=scales[:, cols],

@@ -31,9 +31,10 @@ ROWS = 64
 SERIES_N = N // 2
 GROUP_N = 8
 KS = PASSES * PACK
-SHARE = 256
+SHARE = 224
 LATE = 12
-EVERY = 2
+EVERY = 4
+EARLY = 1
 
 
 def tile_iqnlearnedcosinequantilehead_t_kernel(tc, psi, tau, omega, gc, wc_bytes, wc_scale, bc, wq, out):
@@ -74,25 +75,23 @@ def tile_iqnlearnedcosinequantilehead_t_kernel(tc, psi, tau, omega, gc, wc_bytes
         make_identity(nc, ident[:])
         zero = kept("zero", [P, 1], F32)
         nc.vector.memset(zero[:], 0.0)
-        one = kept("one", [P, 1], F32)
-        nc.vector.memset(one[:], 1.0)
+        ones = kept("ones", [P, TERMS - 1], F32)
+        nc.vector.memset(ones[:], 1.0)
         inv = kept("inv", [P, TERMS], F32)
         nc.scalar.activation(out=inv[:, 0:1], in_=zero[:], func=ACT.Sin)
         half_pi = kept("half_pi", [P, 1], F32)
-        nc.vector.tensor_scalar(out=half_pi[:], in0=one[:], scalar1=math.pi / 2, scalar2=None, op0=ALU.mult)
+        nc.vector.tensor_scalar(out=half_pi[:], in0=ones[:, 0:1], scalar1=math.pi / 2, scalar2=None, op0=ALU.mult)
         seeds = kept("seeds", [P, PASSES * PACK, TERMS], F32)
         nc.vector.memset(seeds[:], 0.0)
         powers = kept("powers", [P, SERIES_N, TERMS], F32)
-        nc.vector.memset(powers[:], 1.0)
+        nc.vector.memset(powers[:, :, 0], 1.0)
         counts = kept("counts", [P, TERMS - 1], F32)
-        ones = powers[:, 0, 1:]
-        nc.vector.tensor_tensor_scan(out=counts[:], data0=ones, data1=ones, initial=0.0, op0=ALU.mult, op1=ALU.add)
-        basis = []
-        for j in range(2):
-            z = kept("basis%d" % j, [P, 2 * GROUP_N * B], BF16)
-            basis.append(z)
-        nc.vector.memset(basis[0][:].bitcast(I32), 0)
+        nc.vector.tensor_tensor_scan(out=counts[:], data0=ones[:], data1=ones[:], initial=0.0, op0=ALU.mult, op1=ALU.add)
+        stuffed = kept("stuffed", [P, GROUP_N * 2 * ROWS * 2], BF16)
+        nc.vector.memset(stuffed[:].bitcast(I32), 0)
         nc.vector.reciprocal(out=inv[:, 1:], in_=counts[:])
+        ident32 = kept("ident32", [P, P], F32)
+        nc.vector.tensor_copy(out=ident32[:], in_=ident[:])
 
         neg_freq = kept("neg_freq", [P, PASSES * PACK], F32)
         omega_flat = omega_sb[:].rearrange("p g t -> p (g t)")
@@ -102,8 +101,10 @@ def tile_iqnlearnedcosinequantilehead_t_kernel(tc, psi, tau, omega, gc, wc_bytes
 
         def spread_tau(n0):
             ps = bank("tau", [P, GROUP_N * B], BF16)
-            for j in range(GROUP_N):
-                nc.tensor.transpose(ps[:, j * B:(j + 1) * B], tau_sb[:, n0 + j:n0 + j + 1].to_broadcast([P, P]), ident[:])
+            for j in range(GROUP_N // 2):
+                w = n0 // 2 + j
+                nc.tensor.transpose(ps[:].bitcast(F32)[:, j * B:(j + 1) * B], tau_sb[:].bitcast(F32)[:, w:w + 1].to_broadcast([P, P]),
+                                    ident32[:])
             tiles["tau", n0] = ps
 
         def cosine(index):
@@ -111,7 +112,8 @@ def tile_iqnlearnedcosinequantilehead_t_kernel(tc, psi, tau, omega, gc, wc_bytes
             g, t = divmod(k, PACK)
             if t == 0:
                 tiles["cos", n0, g] = staged("cos", "cos", [P, PACK, GROUP_N * B], F32, 4)
-            nc.scalar.activation(out=tiles["cos", n0, g][:, t, :], in_=tiles["tau", n0][:], func=ACT.Sin,
+            nc.scalar.activation(out=tiles["cos", n0, g][:, t, :].rearrange("p (w e b) -> p w e b", e=2, b=B),
+                                 in_=tiles["tau", n0][:].rearrange("p (w b e) -> p w e b", e=2, b=B), func=ACT.Sin,
                                  scale=neg_freq[:, k:k + 1], bias=half_pi[:])
             if k == KS - 1 and n0 + GROUP_N < SERIES_N:
                 spread_tau(n0 + GROUP_N)
@@ -146,9 +148,9 @@ def tile_iqnlearnedcosinequantilehead_t_kernel(tc, psi, tau, omega, gc, wc_bytes
         def series_matmuls(n0, g, half):
             ps = bank("series", [P, TOK // 2, 2, 2], BF16)
             first = (n0 - SERIES_N) * B + half * (TOK // 2)
-            z = basis[first // (GROUP_N * B) % 2]
+            z = tiles["basis", first // (GROUP_N * B)]
             first = first % (GROUP_N * B)
-            moving = z[:].rearrange("p (h x) -> p x h", h=2)[:, first:first + TOK // 2, :]
+            moving = z[:, 2 * first:2 * first + TOK].rearrange("p (x h) -> p x h", h=2)
             for u in range(2):
                 nc.tensor.matmul(ps[:, :, u, :], lhsT=coef[:, g * 2 + u, :], rhs=moving, start=True, stop=True)
             tiles["series", n0, g, half] = ps
@@ -214,7 +216,6 @@ def tile_iqnlearnedcosinequantilehead_t_kernel(tc, psi, tau, omega, gc, wc_bytes
         trig = kept("trig", [P, KS, 4], F32)
         nc.scalar.activation(out=trig[:, :, 0], in_=neg_freq[:], func=ACT.Sin, scale=0.5, bias=half_pi[:])
         nc.scalar.activation(out=trig[:, :, 1], in_=neg_freq[:], func=ACT.Sin, scale=0.5)
-        nc.scalar.copy(out=basis[1][:], in_=basis[0][:])
         spread_tau(0)
         psi_ps = bank("psi", [P, B // RUN, PACK, RUN], BF16)
         for t in range(PACK):
@@ -261,9 +262,8 @@ def tile_iqnlearnedcosinequantilehead_t_kernel(tc, psi, tau, omega, gc, wc_bytes
         assert r5.stop == ROWS
         a_rows = kept("a_rows", [P, KS, ROWS], BF16)
         a_rest = kept("a_rest", [P, KS, MID], F32)
-        b_rows = kept("b_rows", [P, SERIES_N, 2, ROWS], BF16)
+        b_top = kept("b_rows", [P, SERIES_N, ROWS], BF16)
         b_rest = kept("b_rest", [P, SERIES_N, MID - 1], F32)
-        b_top = b_rows[:, :, 0, :]
         nc.vector.tensor_copy(out=a_rows[:, :, r0], in_=terms[:])
         nc.vector.tensor_copy(out=b_top[:, :, r0], in_=powers[:])
         nc.vector.tensor_tensor(out=a_rest[:], in0=terms[:, :, 0:MID], in1=a_rows[:, :, 0:MID], op=ALU.subtract)
@@ -279,6 +279,11 @@ def tile_iqnlearnedcosinequantilehead_t_kernel(tc, psi, tau, omega, gc, wc_bytes
         nc.vector.tensor_copy(out=b_top[:, :, r3], in_=powers[:, :, 0:LOW])
         nc.vector.tensor_copy(out=b_top[:, :, r4], in_=b_rest[:, :, 0:LOW - 1])
 
+        def stuff(j):
+            view = stuffed[:].rearrange("p (n h r e) -> p n h r e", h=2, r=ROWS, e=2)
+            for h in range(2):
+                nc.vector.tensor_copy(out=view[:, :, h, :, h], in_=b_top[:, j * GROUP_N:(j + 1) * GROUP_N, :])
+
         wides = []
         for g in range(PASSES):
             wide = kept("wc_wide%d" % g, [P, PACK, D], BF16)
@@ -286,7 +291,7 @@ def tile_iqnlearnedcosinequantilehead_t_kernel(tc, psi, tau, omega, gc, wc_bytes
                 nc.vector.tensor_scalar(out=wide[:, t, :], in0=wc_raw[:, g, t * D:(t + 1) * D].bitcast(FP8),
                                         scalar1=wc_scale_sb[:, g, t:t + 1], scalar2=None, op0=ALU.mult)
                 if g == 0 and t == 0:
-                    nc.vector.tensor_copy(out=b_rows[:, :, 1, :], in_=b_top)
+                    stuff(0)
             wides.append(wide)
         grouped = []
         for g in range(PASSES):
@@ -307,14 +312,16 @@ def tile_iqnlearnedcosinequantilehead_t_kernel(tc, psi, tau, omega, gc, wc_bytes
             nc.tensor.transpose(coef_ps[:, k, :], a_rows[:, 2 * k:2 * k + 2, :].rearrange("p h r -> p (h r)"), ident[:])
 
         def turn_basis(j):
-            ps = bank("series", [P, GROUP_N * B], BF16)
-            for n in range(GROUP_N):
-                nc.tensor.transpose(ps[:, n * B:(n + 1) * B], b_rows[:, j * GROUP_N + n, :, :].rearrange("p h r -> p (h r)"), ident[:])
-            tiles["basis"] = ps
+            tiles["basis", j] = staged("basis", "basis", [P, GROUP_N * B * 2], BF16, 2)
+            for half in range(2):
+                ps = bank("series", [P, TOK * 2], BF16)
+                for n in range(TILE_N):
+                    w = (half * TILE_N + n) * P
+                    nc.tensor.transpose(ps[:].bitcast(F32)[:, n * B:(n + 1) * B], stuffed[:].bitcast(F32)[:, w:w + P], ident32[:])
+                tiles["turned", half] = ps
 
-        def basis_out(j, h, copy):
-            rows = slice(h * ROWS, (h + 1) * ROWS)
-            copy(out=basis[j % 2][rows, h * GROUP_N * B:(h + 1) * GROUP_N * B], in_=tiles["basis"][rows, :])
+        def basis_out(j, half):
+            nc.scalar.copy(out=tiles["basis", j][:, half * TOK * 2:(half + 1) * TOK * 2].bitcast(F32), in_=tiles["turned", half][:].bitcast(F32))
 
         def unit(u):
             return SERIES_N + u // PASSES * TILE_N, u % PASSES
@@ -326,8 +333,8 @@ def tile_iqnlearnedcosinequantilehead_t_kernel(tc, psi, tau, omega, gc, wc_bytes
 
         turn_basis(0)
         nc.scalar.copy(out=coef[:], in_=coef_ps[:])
-        basis_out(0, 0, nc.scalar.copy)
-        basis_out(0, 1, nc.scalar.copy)
+        basis_out(0, 0)
+        basis_out(0, 1)
         for u in range(3):
             for half in range(2):
                 series_matmuls(*unit(u), half)
@@ -337,6 +344,7 @@ def tile_iqnlearnedcosinequantilehead_t_kernel(tc, psi, tau, omega, gc, wc_bytes
         for half in range(2):
             series_matmuls(*unit(3), half)
         quantise_c(SERIES_N, 0)
+        stuff(1)
         features_tile(0, 0)
         gain(0, 0, 0)
         quantise_c(SERIES_N, 1)
@@ -358,39 +366,43 @@ def tile_iqnlearnedcosinequantilehead_t_kernel(tc, psi, tau, omega, gc, wc_bytes
             u = s + 3
             share = -(-len(sines) // (SINE_STEPS - s)) if s < SINE_STEPS else 0
             turn = u + 1 < UNITS and (u + 1) % 4 == 0
-            gain_on_gpsimd(*gain_unit(s + 2), SHARE)
+            shared = SHARE if s > 0 else 0
+            if shared:
+                gain_on_gpsimd(*gain_unit(s + 2), shared)
+            else:
+                features_tile(*gain_unit(s + 2), "c_shared", 1)
             if done is not None:
                 second_matmul(done, 0)
             for t in range(PACK - 1):
                 first_matmul(now, t)
             if u < UNITS:
-                series_out(*unit(u), 0, nc.vector.tensor_copy if 0 < s < LATE and s % EVERY == 0 else nc.scalar.copy)
+                series_out(*unit(u), 0, nc.vector.tensor_copy if EARLY <= s < LATE and s % EVERY == 0 else nc.scalar.copy)
                 series_out(*unit(u), 1, nc.vector.tensor_copy if 0 < s < LATE else nc.scalar.copy)
             if last is not None:
                 modulate(last)
+            if turn:
+                turn_basis((u + 1) // 4)
+            next_sines(min(share, 1))
             if done is not None:
                 store(done, 0, "scalar")
                 second_matmul(done, 1)
-            if turn:
-                turn_basis((u + 1) // 4)
-            elif u + 1 < UNITS:
-                series_matmuls(*unit(u + 1), 0)
-                series_matmuls(*unit(u + 1), 1)
-            next_sines(min(share, 1))
             bias_relu(now, 0)
             first_matmul(now, 3)
             if turn:
-                basis_out((u + 1) // 4, 0, nc.scalar.copy)
-                basis_out((u + 1) // 4, 1, nc.scalar.copy)
+                basis_out((u + 1) // 4, 0)
+                basis_out((u + 1) // 4, 1)
+            if u + 1 < UNITS:
                 series_matmuls(*unit(u + 1), 0)
                 series_matmuls(*unit(u + 1), 1)
             bias_relu(now, 1)
+            bias_relu(now, 2)
             if done is not None:
                 store(done, 1, "scalar")
-            bias_relu(now, 2)
             bias_relu(now, 3)
             next_sines(max(share - 1, 0))
-            gain(*gain_unit(s + 2), SHARE)
+            gain(*gain_unit(s + 2), shared)
+            if turn and u + 5 < UNITS:
+                stuff((u + 5) // 4)
             if last is not None:
                 quantise_m(last)
             quantise_c(*unit(s + 2))

@@ -20,21 +20,27 @@ ACT = mybir.ActivationFunctionType
 P = 128
 PACK = 4
 PASSES = E // (P * PACK)
+PLANES = PASSES * PACK
 TILE_N = 4
 TOK = TILE_N * B
 TILES = N // TILE_N
-RUN = 2
-TERMS = 20
-MID = 13
-LOW = 7
-ROWS = 64
+GROUP_N = 2 * TILE_N
 SERIES_N = N // 2
-GROUP_N = 8
-KS = PASSES * PACK
-SHARE = 224
-LATE = 12
-EVERY = 4
-EARLY = 1
+UNITS = SERIES_N // TILE_N * PASSES
+GROUP_UNITS = GROUP_N // TILE_N * PASSES
+RUN = 2
+RUN_BF16 = 4
+
+TERMS, MID, LOW = 20, 13, 7
+ROWS = P // 2
+TRIG = 4
+
+GPSIMD_ONE_COPY, GPSIMD_TWO_COPIES, GPSIMD_NO_COPY = 208, 272, 176
+SCALAR_SHARE = 160
+FIRST_SINES = 6
+OUT_LEAD = 3
+
+PSUM_BANKS = {"tau": 1, "psi": 1, "series": 2, "first": 3, "second": 1}
 
 
 def tile_iqnlearnedcosinequantilehead_t_kernel(tc, psi, tau, omega, gc, wc_bytes, wc_scale, bc, wq, out):
@@ -52,7 +58,9 @@ def tile_iqnlearnedcosinequantilehead_t_kernel(tc, psi, tau, omega, gc, wc_bytes
             return work.tile(shape, dtype, name=name, tag=tag, bufs=bufs, align_bytes=64)
 
         def bank(tag, shape, dtype):
-            return psum.tile(shape, dtype, name=tag, tag=tag, bufs={"tau": 1, "psi": 1, "series": 2, "first": 3, "second": 1}[tag])
+            return psum.tile(shape, dtype, name=tag, tag=tag, bufs=PSUM_BANKS[tag])
+
+        tiles = {}
 
         tau_sb = kept("tau_sb", [P, N], BF16)
         omega_sb = kept("omega_sb", [P, PASSES, PACK], BF16)
@@ -81,7 +89,7 @@ def tile_iqnlearnedcosinequantilehead_t_kernel(tc, psi, tau, omega, gc, wc_bytes
         nc.scalar.activation(out=inv[:, 0:1], in_=zero[:], func=ACT.Sin)
         half_pi = kept("half_pi", [P, 1], F32)
         nc.vector.tensor_scalar(out=half_pi[:], in0=ones[:, 0:1], scalar1=math.pi / 2, scalar2=None, op0=ALU.mult)
-        seeds = kept("seeds", [P, PASSES * PACK, TERMS], F32)
+        seeds = kept("seeds", [P, PLANES, TERMS], F32)
         nc.vector.memset(seeds[:], 0.0)
         powers = kept("powers", [P, SERIES_N, TERMS], F32)
         nc.vector.memset(powers[:, :, 0], 1.0)
@@ -93,72 +101,113 @@ def tile_iqnlearnedcosinequantilehead_t_kernel(tc, psi, tau, omega, gc, wc_bytes
         ident32 = kept("ident32", [P, P], F32)
         nc.vector.tensor_copy(out=ident32[:], in_=ident[:])
 
-        neg_freq = kept("neg_freq", [P, PASSES * PACK], F32)
+        neg_freq = kept("neg_freq", [P, PLANES], F32)
         omega_flat = omega_sb[:].rearrange("p g t -> p (g t)")
         nc.vector.scalar_tensor_tensor(out=neg_freq[:], in0=omega_flat, scalar=-1.0, in1=omega_flat, op0=ALU.mult, op1=ALU.min)
-
-        tiles = {}
 
         def spread_tau(n0):
             ps = bank("tau", [P, GROUP_N * B], BF16)
             for j in range(GROUP_N // 2):
                 w = n0 // 2 + j
-                nc.tensor.transpose(ps[:].bitcast(F32)[:, j * B:(j + 1) * B], tau_sb[:].bitcast(F32)[:, w:w + 1].to_broadcast([P, P]),
-                                    ident32[:])
+                column = tau_sb[:].bitcast(F32)[:, w:w + 1].to_broadcast([P, P])
+                nc.tensor.transpose(ps[:].bitcast(F32)[:, j * B:(j + 1) * B], column, ident32[:])
             tiles["tau", n0] = ps
 
         def cosine(index):
-            n0, k = index // KS * GROUP_N, index % KS
-            g, t = divmod(k, PACK)
+            n0, plane = index // PLANES * GROUP_N, index % PLANES
+            g, t = divmod(plane, PACK)
             if t == 0:
-                tiles["cos", n0, g] = staged("cos", "cos", [P, PACK, GROUP_N * B], F32, 4)
+                tiles["cos", n0, g] = staged("cos", "cos", [P, PACK, GROUP_N * B], F32, 2 * PASSES)
             nc.scalar.activation(out=tiles["cos", n0, g][:, t, :].rearrange("p (w e b) -> p w e b", e=2, b=B),
                                  in_=tiles["tau", n0][:].rearrange("p (w b e) -> p w e b", e=2, b=B), func=ACT.Sin,
-                                 scale=neg_freq[:, k:k + 1], bias=half_pi[:])
-            if k == KS - 1 and n0 + GROUP_N < SERIES_N:
+                                 scale=neg_freq[:, plane:plane + 1], bias=half_pi[:])
+            if plane == PLANES - 1 and n0 + GROUP_N < SERIES_N:
                 spread_tau(n0 + GROUP_N)
 
-        def walk_planes(planes):
-            return planes.rearrange("p t (c i) -> p c t i", i=RUN)
+        sines = list(range(SERIES_N // GROUP_N * PLANES))
 
-        def walk_words(flat):
-            return flat.rearrange("p (c i t) -> p c t i", i=RUN, t=PACK)
+        def next_sines(count):
+            for index in sines[:count]:
+                cosine(index)
+                sines.remove(index)
 
-        def features_tile(n0, g, tag="c", bufs=5):
-            c = staged("c_%d_%d" % (n0, g), tag, [P, TOK * PACK], BF16, bufs)
-            tiles["c", n0, g] = c
-            return c
+        def sine_unit(u):
+            return u // PASSES * TILE_N, u % PASSES
+
+        def features_tile(n0, g, tag, bufs):
+            tiles["c", n0, g] = staged("c_%d_%d" % (n0, g), tag, [P, TOK * PACK], BF16, bufs)
+
+        def copied_features_tile(n0, g):
+            features_tile(n0, g, "c", 5)
+
+        def shared_features_tile(n0, g):
+            features_tile(n0, g, "c_shared", 1)
 
         def cos_planes(n0, g, first, count):
-            first = first + n0 % GROUP_N * B
-            return tiles["cos", n0 - n0 % GROUP_N, g][:, :, first:first + count]
+            start = first + n0 % GROUP_N * B
+            return tiles["cos", n0 - n0 % GROUP_N, g][:, :, start:start + count]
 
-        def gain(n0, g, first):
+        def gain_on_vector(n0, g, first):
             count = TOK - first
             gains = gc_sb[:, g, :].unsqueeze(1).unsqueeze(3).to_broadcast([P, count // RUN, PACK, RUN])
-            nc.vector.tensor_tensor(out=walk_words(tiles["c", n0, g][:, first * PACK:]), in0=walk_planes(cos_planes(n0, g, first, count)),
+            nc.vector.tensor_tensor(out=tiles["c", n0, g][:, first * PACK:].rearrange("p (c i t) -> p c t i", i=RUN, t=PACK),
+                                    in0=cos_planes(n0, g, first, count).rearrange("p t (c i) -> p c t i", i=RUN),
                                     in1=gains, op=ALU.mult)
 
         def gain_on_gpsimd(n0, g, count):
-            c = features_tile(n0, g, "c_shared", 1)
-            nc.gpsimd.tensor_tensor(out=c[:, :count * PACK].rearrange("p (x t) -> p x t", t=PACK),
+            nc.gpsimd.tensor_tensor(out=tiles["c", n0, g][:, :count * PACK].rearrange("p (x t) -> p x t", t=PACK),
                                     in0=cos_planes(n0, g, 0, count).rearrange("p t x -> p x t"),
                                     in1=gc_sb[:, g, :].unsqueeze(1).to_broadcast([P, count, PACK]), op=ALU.mult)
 
-        def series_matmuls(n0, g, half):
-            ps = bank("series", [P, TOK // 2, 2, 2], BF16)
-            first = (n0 - SERIES_N) * B + half * (TOK // 2)
-            z = tiles["basis", first // (GROUP_N * B)]
-            first = first % (GROUP_N * B)
-            moving = z[:, 2 * first:2 * first + TOK].rearrange("p (x h) -> p x h", h=2)
-            for u in range(2):
-                nc.tensor.matmul(ps[:, :, u, :], lhsT=coef[:, g * 2 + u, :], rhs=moving, start=True, stop=True)
-            tiles["series", n0, g, half] = ps
+        def gain_on_scalar(n0, g, first):
+            planes = staged("gained", "gained", [P, PACK, SCALAR_SHARE], BF16, 2)
+            cos = cos_planes(n0, g, first, SCALAR_SHARE)
+            for t in range(PACK):
+                nc.scalar.activation(out=planes[:, t, :], in_=cos[:, t, :], func=ACT.Copy, scale=seeds[:, g * PACK + t, 0:1])
+            tiles["gained"] = planes
+
+        def interleave_on_scalar(n0, g, first):
+            words = tiles["c", n0, g][:, first * PACK:(first + SCALAR_SHARE) * PACK]
+            nc.scalar.copy(out=words.rearrange("p (c i t) -> p c t i", i=RUN_BF16, t=PACK),
+                           in_=tiles["gained"][:].rearrange("p t (c i) -> p c t i", i=RUN_BF16))
+
+        def series_unit(u):
+            return SERIES_N + u // PASSES * TILE_N, u % PASSES
+
+        def stuff(group):
+            view = stuffed[:].rearrange("p (n h r e) -> p n h r e", h=2, r=ROWS, e=2)
+            for h in range(2):
+                nc.vector.tensor_copy(out=view[:, :, h, :, h], in_=power_rows[:, group * GROUP_N:(group + 1) * GROUP_N, :])
+
+        def turn_basis(group):
+            tiles["basis", group] = staged("basis", "basis", [P, GROUP_N * B * 2], BF16, 2)
+            for half in range(2):
+                ps = bank("series", [P, TOK * 2], BF16)
+                for n in range(TILE_N):
+                    w = (half * TILE_N + n) * P
+                    nc.tensor.transpose(ps[:].bitcast(F32)[:, n * B:(n + 1) * B], stuffed[:].bitcast(F32)[:, w:w + P], ident32[:])
+                tiles["turned", half] = ps
+
+        def basis_out(group):
+            for half in range(2):
+                nc.scalar.copy(out=tiles["basis", group][:, half * TOK * 2:(half + 1) * TOK * 2].bitcast(F32),
+                               in_=tiles["turned", half][:].bitcast(F32))
+
+        def series_matmuls(n0, g):
+            for half in range(2):
+                ps = bank("series", [P, TOK // 2, 2, 2], BF16)
+                group, first = divmod((n0 - SERIES_N) * B + half * (TOK // 2), GROUP_N * B)
+                moving = tiles["basis", group][:, 2 * first:2 * first + TOK].rearrange("p (x h) -> p x h", h=2)
+                for u in range(2):
+                    nc.tensor.matmul(ps[:, :, u, :], lhsT=coef[:, g * 2 + u, :], rhs=moving, start=True, stop=True)
+                tiles["series", n0, g, half] = ps
 
         def series_out(n0, g, half, copy):
-            c = features_tile(n0, g) if half == 0 else tiles["c", n0, g]
+            if half == 0:
+                copied_features_tile(n0, g)
             width = TOK * PACK // 2
-            copy(out=c[:, half * width:(half + 1) * width], in_=tiles["series", n0, g, half][:].rearrange("p x u h -> p (x u h)"))
+            copy(out=tiles["c", n0, g][:, half * width:(half + 1) * width],
+                 in_=tiles["series", n0, g, half][:].rearrange("p x u h -> p (x u h)"))
 
         def quantise(name, source, width, bufs):
             codes = staged(name + "_codes", name + "_codes", [P, width], U32, bufs)
@@ -169,297 +218,251 @@ def tile_iqnlearnedcosinequantilehead_t_kernel(tc, psi, tau, omega, gc, wc_bytes
         def quantise_c(n0, g):
             tiles["cq", n0, g] = quantise("c", tiles["c", n0, g][:], TOK, 9)
 
-        def first_matmul(n0, t):
-            ps = bank("first", [P, TOK], F32)
+        def first_passes(ps, n0, t, tokens):
             cols = slice(t * P, (t + 1) * P)
             for g in range(PASSES):
                 codes, scales = tiles["cq", n0, g]
-                nc.tensor.matmul_mx(out=ps[:], lhsT=wc_q[g][0][:, cols].bitcast(FP8X4), lhsT_scale=wc_q[g][1][:, cols],
-                                    rhs=codes[:].bitcast(FP8X4), rhs_scale=scales[:], start=(g == 0), stop=(g == PASSES - 1))
+                nc.tensor.matmul_mx(out=ps, lhsT=wc_q[g][0][:, cols].bitcast(FP8X4), lhsT_scale=wc_q[g][1][:, cols],
+                                    rhs=codes[:, tokens].bitcast(FP8X4), rhs_scale=scales[:, tokens],
+                                    start=(g == 0), stop=(g == PASSES - 1))
+
+        def first_matmul(n0, t):
+            ps = bank("first", [P, TOK], F32)
+            first_passes(ps[:], n0, t, slice(0, TOK))
             tiles["first", n0, t] = ps
+
+        def phi_tile(n0):
+            tiles["phi", n0] = staged("phi", "phi", [P, PACK, TOK], F32, 2)
 
         def bias_relu(n0, t):
             if t == 0:
-                tiles["phi", n0] = staged("phi", "phi", [P, PACK, TOK], F32, 3)
+                phi_tile(n0)
             nc.scalar.activation(out=tiles["phi", n0][:, t, :], in_=tiles["first", n0, t][:], func=ACT.Relu, bias=bc_sb[:, t:t + 1])
 
-        def times_psi(words, planes, count):
-            nc.vector.tensor_tensor(out=words.rearrange("p (n c i t) -> p n c t i", n=count, i=RUN, t=PACK),
+        M_BUFS = 4
+
+        def modulate(n0, first, count):
+            m = staged("m", "m", [P, count * B * PACK], BF16, M_BUFS)
+            planes = tiles["phi", n0][:, :, first * B:(first + count) * B]
+            nc.vector.tensor_tensor(out=m[:].rearrange("p (n c i t) -> p n c t i", n=count, i=RUN, t=PACK),
                                     in0=planes.rearrange("p t (n c i) -> p n c t i", n=count, i=RUN),
                                     in1=psi_ps[:].unsqueeze(1).to_broadcast([P, count, B // RUN, PACK, RUN]), op=ALU.mult)
+            tiles["m", n0, first] = m
 
-        def modulate(n0):
-            m = staged("m", "m", [P, TOK * PACK], BF16, 3)
-            times_psi(m[:], tiles["phi", n0][:], TILE_N)
-            tiles["m", n0] = m
+        def quantise_m(n0, first, count):
+            codes, scales = quantise("m", tiles["m", n0, first][:], count * B, M_BUFS)
+            for j in range(count):
+                cols = slice(j * B, (j + 1) * B)
+                tiles["mq", n0 + first + j] = codes[:, cols], scales[:, cols]
 
-        def quantise_m(n0):
-            tiles["mq", n0] = quantise("m", tiles["m", n0][:], TOK, 3)
-
-        def second_matmul(n0, half, tag="second"):
-            ps = bank(tag, [P, 2, A], F32)
-            codes, scales = tiles["mq", n0]
-            for j in range(2):
-                cols = slice((half * 2 + j) * B, (half * 2 + j + 1) * B)
-                nc.tensor.matmul_mx(out=ps[:, j, :], lhsT=codes[:, cols].bitcast(FP8X4), lhsT_scale=scales[:, cols],
+        def second_matmul(n, count, tag):
+            ps = bank(tag, [P, count, A], F32)
+            for j in range(count):
+                codes, scales = tiles["mq", n + j]
+                nc.tensor.matmul_mx(out=ps[:, j, :], lhsT=codes.bitcast(FP8X4), lhsT_scale=scales,
                                     rhs=wq_q[0][:].bitcast(FP8X4), rhs_scale=wq_q[1][:], start=True, stop=True)
-            tiles["second", n0, half] = ps
+            tiles["second", n] = ps
 
-        def store(n0, half, engine):
-            res = staged("res", "res", [P, 2, A], F32, 6)
-            if engine == "scalar":
-                nc.scalar.copy(out=res[:], in_=tiles["second", n0, half][:])
-            else:
-                nc.vector.tensor_copy(out=res[:], in_=tiles["second", n0, half][:])
-            nc.sync.dma_start(out=out[:, n0 + half * 2:n0 + half * 2 + 2, :], in_=res[:])
+        def store(n, count, copy):
+            res = staged("res", "res", [P, count, A], F32, 6)
+            copy(out=res[:], in_=tiles["second", n][:])
+            nc.sync.dma_start(out=out[:, n:n + count, :], in_=res[:])
 
-        trig = kept("trig", [P, KS, 4], F32)
+        trig = kept("trig", [P, PLANES, TRIG], F32)
         nc.scalar.activation(out=trig[:, :, 0], in_=neg_freq[:], func=ACT.Sin, scale=0.5, bias=half_pi[:])
         nc.scalar.activation(out=trig[:, :, 1], in_=neg_freq[:], func=ACT.Sin, scale=0.5)
         spread_tau(0)
         psi_ps = bank("psi", [P, B // RUN, PACK, RUN], BF16)
         for t in range(PACK):
             nc.tensor.transpose(psi_ps[:, :, t, :], psi_sb[:, t::PACK], ident[:])
-        sines = list(range(SERIES_N // GROUP_N * KS))
+        next_sines(FIRST_SINES)
 
-        def next_sines(count):
-            for index in sines[:count]:
-                cosine(index)
-                sines.remove(index)
-
-        next_sines(6)
-
-        steps = kept("steps", [P, KS, TERMS], F32)
-        scaled = kept("scaled", [P, KS, TERMS], F32)
-        terms = kept("terms", [P, KS, TERMS], F32)
-        nc.vector.tensor_scalar(out=powers[:, :, 1], in0=tau_sb[:, SERIES_N:], scalar1=2.0, scalar2=-1.0, op0=ALU.mult, op1=ALU.add)
-        nc.vector.scalar_tensor_tensor(out=steps[:], in0=neg_freq[:].unsqueeze(2).to_broadcast([P, KS, TERMS]), scalar=-0.5,
-                                       in1=inv[:].unsqueeze(1).to_broadcast([P, KS, TERMS]), op0=ALU.mult, op1=ALU.mult)
+        ratios = kept("ratios", [P, PLANES, TERMS], F32)
+        scaled = kept("scaled", [P, PLANES, TERMS], F32)
+        terms = kept("terms", [P, PLANES, TERMS], F32)
 
         def double_powers(top):
             more = min(top, TERMS - 1 - top)
             nc.vector.tensor_tensor(out=powers[:, :, top + 1:top + 1 + more], in0=powers[:, :, 1:1 + more],
                                     in1=powers[:, :, top:top + 1].to_broadcast([P, SERIES_N, more]), op=ALU.mult)
 
+        nc.vector.tensor_scalar(out=powers[:, :, 1], in0=tau_sb[:, SERIES_N:], scalar1=2.0, scalar2=-1.0, op0=ALU.mult, op1=ALU.add)
+        nc.vector.scalar_tensor_tensor(out=ratios[:], in0=neg_freq[:].unsqueeze(2).to_broadcast([P, PLANES, TERMS]), scalar=-0.5,
+                                       in1=inv[:].unsqueeze(1).to_broadcast([P, PLANES, TERMS]), op0=ALU.mult, op1=ALU.mult)
         double_powers(1)
         nc.vector.tensor_copy(out=seeds[:, :, 0], in_=gc_sb[:].rearrange("p g t -> p (g t)"))
         double_powers(2)
         nc.vector.tensor_scalar(out=trig[:, :, 2:4], in0=trig[:, :, 0:2], scalar1=-1.0, scalar2=None, op0=ALU.mult)
         double_powers(4)
-        nc.vector.tensor_tensor_scan(out=scaled[:].rearrange("p k j -> p (k j)"), data0=steps[:].rearrange("p k j -> p (k j)"),
+        nc.vector.tensor_tensor_scan(out=scaled[:].rearrange("p k j -> p (k j)"), data0=ratios[:].rearrange("p k j -> p (k j)"),
                                      data1=seeds[:].rearrange("p k j -> p (k j)"), initial=0.0, op0=ALU.mult, op1=ALU.add)
         double_powers(8)
-        nc.vector.tensor_tensor(out=terms[:].rearrange("p k (a b) -> p k a b", b=4), in0=scaled[:].rearrange("p k (a b) -> p k a b", b=4),
-                                in1=trig[:].unsqueeze(2).to_broadcast([P, KS, TERMS // 4, 4]), op=ALU.mult)
+        nc.vector.tensor_tensor(out=terms[:].rearrange("p k (a b) -> p k a b", b=TRIG),
+                                in0=scaled[:].rearrange("p k (a b) -> p k a b", b=TRIG),
+                                in1=trig[:].unsqueeze(2).to_broadcast([P, PLANES, TERMS // TRIG, TRIG]), op=ALU.mult)
         double_powers(16)
 
-        r0 = slice(0, TERMS)
-        r1 = slice(r0.stop, r0.stop + MID)
-        r2 = slice(r1.stop, r1.stop + MID - 1)
-        r3 = slice(r2.stop, r2.stop + LOW)
-        r4 = slice(r3.stop, r3.stop + LOW - 1)
-        r5 = slice(r4.stop, r4.stop + LOW - 1)
-        assert r5.stop == ROWS
-        a_rows = kept("a_rows", [P, KS, ROWS], BF16)
-        a_rest = kept("a_rest", [P, KS, MID], F32)
-        b_top = kept("b_rows", [P, SERIES_N, ROWS], BF16)
-        b_rest = kept("b_rest", [P, SERIES_N, MID - 1], F32)
-        nc.vector.tensor_copy(out=a_rows[:, :, r0], in_=terms[:])
-        nc.vector.tensor_copy(out=b_top[:, :, r0], in_=powers[:])
-        nc.vector.tensor_tensor(out=a_rest[:], in0=terms[:, :, 0:MID], in1=a_rows[:, :, 0:MID], op=ALU.subtract)
-        nc.vector.tensor_tensor(out=b_rest[:], in0=powers[:, :, 1:MID], in1=b_top[:, :, 1:MID], op=ALU.subtract)
-        nc.vector.tensor_copy(out=a_rows[:, :, r1], in_=a_rest[:])
-        nc.vector.tensor_copy(out=b_top[:, :, r2], in_=b_rest[:])
-        nc.vector.tensor_copy(out=a_rows[:, :, r2], in_=terms[:, :, 1:MID])
-        nc.vector.tensor_tensor(out=a_rows[:, :, r3], in0=a_rest[:, :, 0:LOW], in1=a_rows[:, :, r1.start:r1.start + LOW], op=ALU.subtract)
-        nc.vector.tensor_tensor(out=b_top[:, :, r5], in0=b_rest[:, :, 0:LOW - 1], in1=b_top[:, :, r2.start:r2.start + LOW - 1], op=ALU.subtract)
-        nc.vector.tensor_copy(out=a_rows[:, :, r4], in_=a_rest[:, :, 1:LOW])
-        nc.vector.tensor_copy(out=a_rows[:, :, r5], in_=terms[:, :, 1:LOW])
-        nc.vector.tensor_copy(out=b_top[:, :, r1], in_=powers[:, :, 0:MID])
-        nc.vector.tensor_copy(out=b_top[:, :, r3], in_=powers[:, :, 0:LOW])
-        nc.vector.tensor_copy(out=b_top[:, :, r4], in_=b_rest[:, :, 0:LOW - 1])
+        high_high = slice(0, TERMS)
+        mid_high = slice(high_high.stop, high_high.stop + MID)
+        high_mid = slice(mid_high.stop, mid_high.stop + MID - 1)
+        low_high = slice(high_mid.stop, high_mid.stop + LOW)
+        mid_mid = slice(low_high.stop, low_high.stop + LOW - 1)
+        high_low = slice(mid_mid.stop, mid_mid.stop + LOW - 1)
+        assert high_low.stop == ROWS
+        coef_rows = kept("coef_rows", [P, PLANES, ROWS], BF16)
+        coef_rest = kept("coef_rest", [P, PLANES, MID], F32)
+        power_rows = kept("power_rows", [P, SERIES_N, ROWS], BF16)
+        power_rest = kept("power_rest", [P, SERIES_N, MID - 1], F32)
+        nc.vector.tensor_copy(out=coef_rows[:, :, high_high], in_=terms[:])
+        nc.vector.tensor_copy(out=power_rows[:, :, high_high], in_=powers[:])
+        nc.vector.tensor_tensor(out=coef_rest[:], in0=terms[:, :, 0:MID], in1=coef_rows[:, :, 0:MID], op=ALU.subtract)
+        nc.vector.tensor_tensor(out=power_rest[:], in0=powers[:, :, 1:MID], in1=power_rows[:, :, 1:MID], op=ALU.subtract)
+        nc.vector.tensor_copy(out=coef_rows[:, :, mid_high], in_=coef_rest[:])
+        nc.vector.tensor_copy(out=power_rows[:, :, high_mid], in_=power_rest[:])
+        nc.vector.tensor_copy(out=coef_rows[:, :, high_mid], in_=terms[:, :, 1:MID])
+        nc.vector.tensor_tensor(out=coef_rows[:, :, low_high], in0=coef_rest[:, :, 0:LOW],
+                                in1=coef_rows[:, :, mid_high.start:mid_high.start + LOW], op=ALU.subtract)
+        nc.vector.tensor_tensor(out=power_rows[:, :, high_low], in0=power_rest[:, :, 0:LOW - 1],
+                                in1=power_rows[:, :, high_mid.start:high_mid.start + LOW - 1], op=ALU.subtract)
+        nc.vector.tensor_copy(out=coef_rows[:, :, mid_mid], in_=coef_rest[:, :, 1:LOW])
+        nc.vector.tensor_copy(out=coef_rows[:, :, high_low], in_=terms[:, :, 1:LOW])
+        nc.vector.tensor_copy(out=power_rows[:, :, mid_high], in_=powers[:, :, 0:MID])
+        nc.vector.tensor_copy(out=power_rows[:, :, low_high], in_=powers[:, :, 0:LOW])
+        nc.vector.tensor_copy(out=power_rows[:, :, mid_mid], in_=power_rest[:, :, 0:LOW - 1])
 
-        def stuff(j):
-            view = stuffed[:].rearrange("p (n h r e) -> p n h r e", h=2, r=ROWS, e=2)
-            for h in range(2):
-                nc.vector.tensor_copy(out=view[:, :, h, :, h], in_=b_top[:, j * GROUP_N:(j + 1) * GROUP_N, :])
-
-        wides = []
+        wc_planes = []
         for g in range(PASSES):
-            wide = kept("wc_wide%d" % g, [P, PACK, D], BF16)
-            for t in range(PACK):
-                nc.vector.tensor_scalar(out=wide[:, t, :], in0=wc_raw[:, g, t * D:(t + 1) * D].bitcast(FP8),
-                                        scalar1=wc_scale_sb[:, g, t:t + 1], scalar2=None, op0=ALU.mult)
-                if g == 0 and t == 0:
-                    stuff(0)
-            wides.append(wide)
-        grouped = []
+            wc_planes.append(kept("wc_planes%d" % g, [P, PACK, D], BF16))
+
+        def widen(plane):
+            g, t = divmod(plane, PACK)
+            nc.vector.tensor_scalar(out=wc_planes[g][:, t, :], in0=wc_raw[:, g, t * D:(t + 1) * D].bitcast(FP8),
+                                    scalar1=wc_scale_sb[:, g, t:t + 1], scalar2=None, op0=ALU.mult)
+
+        widen(0)
+        stuff(0)
+        for plane in range(1, PLANES):
+            widen(plane)
+        wc_words = []
         for g in range(PASSES):
             words = kept("wc_words%d" % g, [P, D * PACK], BF16)
-            nc.vector.tensor_copy(out=words[:].rearrange("p (t m j) -> p t m j", t=PACK, j=PACK),
-                                  in_=wides[g][:].rearrange("p j (m t) -> p t m j", t=PACK))
-            grouped.append(words)
+            nc.vector.tensor_copy(out=words[:].rearrange("p (o m t) -> p o m t", o=PACK, t=PACK),
+                                  in_=wc_planes[g][:].rearrange("p t (m o) -> p o m t", o=PACK))
+            wc_words.append(words)
         wq_words = kept("wq_words", [P, A, PACK], BF16)
-        nc.vector.tensor_copy(out=wq_words[:], in_=wq_raw[:].rearrange("p j a -> p a j"))
+        nc.vector.tensor_copy(out=wq_words[:], in_=wq_raw[:].rearrange("p t a -> p a t"))
         wc_q = []
         for g in range(PASSES):
-            wc_q.append(quantise("wc", grouped[g][:], D, PASSES))
-        wq_q = quantise("wq", wq_words[:].rearrange("p a j -> p (a j)"), A, 1)
+            wc_q.append(quantise("wc", wc_words[g][:], D, PASSES))
+        wq_q = quantise("wq", wq_words[:].rearrange("p a t -> p (a t)"), A, 1)
 
-        coef = kept("coef", [P, KS // 2, P], BF16)
-        coef_ps = bank("second", [P, KS // 2, P], BF16)
-        for k in range(KS // 2):
-            nc.tensor.transpose(coef_ps[:, k, :], a_rows[:, 2 * k:2 * k + 2, :].rearrange("p h r -> p (h r)"), ident[:])
-
-        def turn_basis(j):
-            tiles["basis", j] = staged("basis", "basis", [P, GROUP_N * B * 2], BF16, 2)
-            for half in range(2):
-                ps = bank("series", [P, TOK * 2], BF16)
-                for n in range(TILE_N):
-                    w = (half * TILE_N + n) * P
-                    nc.tensor.transpose(ps[:].bitcast(F32)[:, n * B:(n + 1) * B], stuffed[:].bitcast(F32)[:, w:w + P], ident32[:])
-                tiles["turned", half] = ps
-
-        def basis_out(j, half):
-            nc.scalar.copy(out=tiles["basis", j][:, half * TOK * 2:(half + 1) * TOK * 2].bitcast(F32), in_=tiles["turned", half][:].bitcast(F32))
-
-        def unit(u):
-            return SERIES_N + u // PASSES * TILE_N, u % PASSES
-
-        def gain_unit(u):
-            if u < 4:
-                return u // 2 * TILE_N, u % 2
-            return u // 4 * GROUP_N + u % 2 * TILE_N, u // 2 % 2
-
+        coef = kept("coef", [P, PLANES // 2, P], BF16)
+        coef_ps = bank("second", [P, PLANES // 2, P], BF16)
+        for pair in range(PLANES // 2):
+            nc.tensor.transpose(coef_ps[:, pair, :], coef_rows[:, 2 * pair:2 * pair + 2, :].rearrange("p h r -> p (h r)"), ident[:])
         turn_basis(0)
         nc.scalar.copy(out=coef[:], in_=coef_ps[:])
-        basis_out(0, 0)
-        basis_out(0, 1)
-        for u in range(3):
-            for half in range(2):
-                series_matmuls(*unit(u), half)
+        basis_out(0)
+
+        for u in range(OUT_LEAD):
+            series_matmuls(*series_unit(u))
             next_sines(1)
             for half in range(2):
-                series_out(*unit(u), half, nc.scalar.copy)
-        for half in range(2):
-            series_matmuls(*unit(3), half)
-        quantise_c(SERIES_N, 0)
+                series_out(*series_unit(u), half, nc.scalar.copy)
+        series_matmuls(*series_unit(OUT_LEAD))
+        quantise_c(*series_unit(0))
         stuff(1)
-        features_tile(0, 0)
-        gain(0, 0, 0)
-        quantise_c(SERIES_N, 1)
-        features_tile(0, 1, "c_shared", 1)
-        gain(0, 1, 0)
-        quantise_c(0, 0)
-        quantise_c(0, 1)
+        copied_features_tile(*sine_unit(0))
+        gain_on_vector(*sine_unit(0), 0)
+        quantise_c(*series_unit(1))
+        quantise_c(*sine_unit(0))
 
         order = []
         for j in range(TILES // 2):
             order.extend([SERIES_N + j * TILE_N, j * TILE_N])
-        order[-2:] = [order[-1], order[-2]]
-        UNITS = TILES
-        SINE_STEPS = 12
-        for s in range(TILES - 2):
+        PAIR = 2
+        for s in range(TILES - 1):
             now = order[s]
-            last = order[s - 1] if s > 0 else None
-            done = order[s - 2] if s > 1 else None
-            u = s + 3
-            share = -(-len(sines) // (SINE_STEPS - s)) if s < SINE_STEPS else 0
-            turn = u + 1 < UNITS and (u + 1) % 4 == 0
-            shared = SHARE if s > 0 else 0
-            if shared:
-                gain_on_gpsimd(*gain_unit(s + 2), shared)
-            else:
-                features_tile(*gain_unit(s + 2), "c_shared", 1)
-            if done is not None:
-                second_matmul(done, 0)
-            for t in range(PACK - 1):
-                first_matmul(now, t)
-            if u < UNITS:
-                series_out(*unit(u), 0, nc.vector.tensor_copy if EARLY <= s < LATE and s % EVERY == 0 else nc.scalar.copy)
-                series_out(*unit(u), 1, nc.vector.tensor_copy if 0 < s < LATE else nc.scalar.copy)
-            if last is not None:
-                modulate(last)
-            if turn:
-                turn_basis((u + 1) // 4)
-            next_sines(min(share, 1))
-            if done is not None:
-                store(done, 0, "scalar")
-                second_matmul(done, 1)
-            bias_relu(now, 0)
-            first_matmul(now, 3)
-            if turn:
-                basis_out((u + 1) // 4, 0)
-                basis_out((u + 1) // 4, 1)
-            if u + 1 < UNITS:
-                series_matmuls(*unit(u + 1), 0)
-                series_matmuls(*unit(u + 1), 1)
-            bias_relu(now, 1)
-            bias_relu(now, 2)
-            if done is not None:
-                store(done, 1, "scalar")
-            bias_relu(now, 3)
-            next_sines(max(share - 1, 0))
-            gain(*gain_unit(s + 2), shared)
-            if turn and u + 5 < UNITS:
-                stuff((u + 5) // 4)
-            if last is not None:
-                quantise_m(last)
-            quantise_c(*unit(s + 2))
-            quantise_c(*gain_unit(s + 2))
+            gained = sine_unit(s + 1)
+            u = s + OUT_LEAD
+            copying = u < UNITS
+            next_group = (u + 1) // GROUP_UNITS
+            turning = u + 1 < UNITS and (u + 1) % GROUP_UNITS == 0
+            vector_copies = 0 if s == 0 or not copying else 2 - s % 2
+            gpsimd_share = 0 if s == 0 else [GPSIMD_NO_COPY, GPSIMD_ONE_COPY, GPSIMD_TWO_COPIES][vector_copies]
+            scalar_share = 0 if copying else SCALAR_SHARE
 
-        a, b, c, d = order[-4:]
-        second_matmul(a, 0)
-        store(a, 0, "scalar")
-        for t in range(PACK - 1):
-            first_matmul(c, t)
-        second_matmul(a, 1)
-        bias_relu(c, 0)
-        first_matmul(c, 3)
-        for t in range(1, PACK):
-            bias_relu(c, t)
-        store(a, 1, "scalar")
-        modulate(b)
-        quantise_m(b)
-        phi = staged("phi", "phi", [P, PACK, TOK], F32, 3)
-        HALF = TOK // 2
+            shared_features_tile(*gained)
+            if gpsimd_share:
+                gain_on_gpsimd(*gained, gpsimd_share)
+            if s > 1:
+                second_matmul(order[s - 2], PAIR, "second")
+            for t in range(PSUM_BANKS["first"]):
+                first_matmul(now, t)
+            if copying:
+                series_out(*series_unit(u), 0, nc.vector.tensor_copy if vector_copies == 2 else nc.scalar.copy)
+                series_out(*series_unit(u), 1, nc.vector.tensor_copy if vector_copies else nc.scalar.copy)
+            if s > 0:
+                modulate(order[s - 1], 0, TILE_N)
+            if turning:
+                turn_basis(next_group)
+            if scalar_share:
+                gain_on_scalar(*gained, gpsimd_share)
+            if sines:
+                next_sines(1)
+            if s > 1:
+                store(order[s - 2], PAIR, nc.scalar.copy)
+                second_matmul(order[s - 2] + PAIR, PAIR, "second")
+            bias_relu(now, 0)
+            first_matmul(now, PACK - 1)
+            if turning:
+                basis_out(next_group)
+            if u + 1 < UNITS:
+                series_matmuls(*series_unit(u + 1))
+            if scalar_share:
+                interleave_on_scalar(*gained, gpsimd_share)
+            for t in range(1, PACK):
+                bias_relu(now, t)
+            if s > 1:
+                store(order[s - 2] + PAIR, PAIR, nc.scalar.copy)
+            if sines:
+                next_sines(1)
+            gain_on_vector(*gained, gpsimd_share + scalar_share)
+            if turning and next_group + 1 < SERIES_N // GROUP_N:
+                stuff(next_group + 1)
+            if s > 0:
+                quantise_m(order[s - 1], 0, TILE_N)
+            if u - 1 < UNITS:
+                quantise_c(*series_unit(u - 1))
+            quantise_c(*gained)
+
+        third_last, second_last, last = order[-3:]
+        phi_tile(last)
+        second_matmul(third_last, PAIR, "series")
+        second_matmul(third_last + PAIR, PAIR, "series")
+        store(third_last, PAIR, nc.scalar.copy)
         for half in range(2):
-            cols = slice(half * HALF, (half + 1) * HALF)
-            for pair in range(2):
-                ps = bank("first", [P, 2, HALF], F32)
+            tokens = slice(half * TOK // 2, (half + 1) * TOK // 2)
+            for t0 in range(0, PACK, 2):
+                ps = bank("first", [P, 2, TOK // 2], F32)
                 for j in range(2):
-                    t = 2 * pair + j
-                    for g in range(PASSES):
-                        codes, scales = tiles["cq", d, g]
-                        nc.tensor.matmul_mx(out=ps[:, j, :], lhsT=wc_q[g][0][:, t * P:(t + 1) * P].bitcast(FP8X4),
-                                            lhsT_scale=wc_q[g][1][:, t * P:(t + 1) * P], rhs=codes[:, cols].bitcast(FP8X4),
-                                            rhs_scale=scales[:, cols], start=(g == 0), stop=(g == PASSES - 1))
+                    first_passes(ps[:, j, :], last, t0 + j, tokens)
                 for j in range(2):
-                    t = 2 * pair + j
-                    nc.scalar.activation(out=phi[:, t, cols], in_=ps[:, j, :], func=ACT.Relu, bias=bc_sb[:, t:t + 1])
-        modulate(c)
-        second_matmul(b, 0, "series")
-        second_matmul(b, 1, "series")
-        store(b, 0, "scalar")
-        store(b, 1, "scalar")
-        ms = []
-        for half in range(2):
-            m = staged("m", "m", [P, HALF * PACK], BF16, 3)
-            times_psi(m[:], phi[:, :, half * HALF:(half + 1) * HALF], 2)
-            ms.append(m)
-            if half == 0:
-                quantise_m(c)
-        second_matmul(c, 0, "series")
-        second_matmul(c, 1, "series")
-        store(c, 0, "scalar")
-        store(c, 1, "scalar")
-        for half in range(2):
-            codes, scales = quantise("m", ms[half][:], HALF, 3)
-            ps = bank("first", [P, 2, A], F32)
-            for j in range(2):
-                cols = slice(j * B, (j + 1) * B)
-                nc.tensor.matmul_mx(out=ps[:, j, :], lhsT=codes[:, cols].bitcast(FP8X4), lhsT_scale=scales[:, cols],
-                                    rhs=wq_q[0][:].bitcast(FP8X4), rhs_scale=wq_q[1][:], start=True, stop=True)
-            tiles["second", d, half] = ps
-        store(d, 0, "scalar")
-        store(d, 1, "vector")
+                    nc.scalar.activation(out=tiles["phi", last][:, t0 + j, tokens], in_=ps[:, j, :], func=ACT.Relu,
+                                         bias=bc_sb[:, t0 + j:t0 + j + 1])
+        store(third_last + PAIR, PAIR, nc.scalar.copy)
+        modulate(second_last, 0, TILE_N)
+        pieces = [(0, 2, nc.scalar.copy), (2, 1, nc.vector.tensor_copy), (3, 1, nc.scalar.copy)]
+        modulate(last, *pieces[0][:2])
+        quantise_m(second_last, 0, TILE_N)
+        second_matmul(second_last, PAIR, "series")
+        second_matmul(second_last + PAIR, PAIR, "series")
+        store(second_last, PAIR, nc.scalar.copy)
+        store(second_last + PAIR, PAIR, nc.scalar.copy)
+        for first, count, copy in pieces[1:]:
+            modulate(last, first, count)
+        for first, count, copy in pieces:
+            quantise_m(last, first, count)
+            second_matmul(last + first, count, "first")
+        for first, count, copy in pieces:
+            store(last + first, count, copy)

@@ -155,9 +155,10 @@ def tile_iqnlearnedcosinequantilehead_t_kernel(tc, psi, tau, omega, gc, wc_bytes
                                     in1=gains, op=ALU.mult)
 
         def gain_on_gpsimd(n0, g, count):
-            nc.gpsimd.tensor_tensor(out=tiles["c", n0, g][:, :count * PACK].rearrange("p (x t) -> p x t", t=PACK),
-                                    in0=cos_planes(n0, g, 0, count).rearrange("p t x -> p x t"),
-                                    in1=gc_sb[:, g, :].unsqueeze(1).to_broadcast([P, count, PACK]), op=ALU.mult)
+            gains = gc_sb[:, g, :].unsqueeze(1).unsqueeze(3).to_broadcast([P, count // RUN, PACK, RUN])
+            nc.gpsimd.tensor_tensor(out=tiles["c", n0, g][:, :count * PACK].rearrange("p (c i t) -> p c t i", i=RUN, t=PACK),
+                                    in0=cos_planes(n0, g, 0, count).rearrange("p t (c i) -> p c t i", i=RUN),
+                                    in1=gains, op=ALU.mult)
 
         def gain_on_scalar(n0, g, first):
             planes = staged("gained", "gained", [P, PACK, SCALAR_SHARE], BF16, 2)

import math
from contextlib import ExitStack

import concourse.mybir as mybir
from concourse.masks import make_identity

B, N, E, D, A = 128, 64, 1024, 512, 256
FLOPS = 2 * B * N * (E * D + D * A)

F32 = mybir.dt.float32
BF16 = mybir.dt.bfloat16
I32 = mybir.dt.int32
U32 = mybir.dt.uint32
U8 = mybir.dt.uint8
FP8 = mybir.dt.float8_e4m3fn
FP8X4 = mybir.dt.float8_e4m3fn_x4
ALU = mybir.AluOpType
ACT = mybir.ActivationFunctionType

P = 128
PACK = 4
PASSES = E // (P * PACK)
PLANES = PASSES * PACK
TILE_N = 4
TOK = TILE_N * B
TILES = N // TILE_N
GROUP_N = 2 * TILE_N
SERIES_N = N // 2
UNITS = SERIES_N // TILE_N * PASSES
GROUP_UNITS = GROUP_N // TILE_N * PASSES
RUN = 2
RUN_BF16 = 4

TERMS, MID, LOW = 20, 13, 7
ROWS = P // 2
TRIG = 4

GPSIMD_ONE_COPY, GPSIMD_TWO_COPIES, GPSIMD_NO_COPY = 208, 272, 176
SCALAR_SHARE = 160
FIRST_SINES = 6
OUT_LEAD = 3

PSUM_BANKS = {"tau": 1, "psi": 1, "series": 2, "first": 3, "second": 1}


def tile_iqnlearnedcosinequantilehead_t_kernel(tc, psi, tau, omega, gc, wc_bytes, wc_scale, bc, wq, out):
    nc = tc.nc
    with ExitStack() as ctx:
        keep = ctx.enter_context(tc.tile_pool(name="keep", bufs=1))
        work = ctx.enter_context(tc.tile_pool(name="work", bufs=2))
        psum = ctx.enter_context(tc.psum_pool(name="psum", bufs=1))
        ctx.enter_context(tc.manual_schedule())

        def kept(name, shape, dtype):
            return keep.tile(shape, dtype, name=name, align_bytes=64)

        def staged(name, tag, shape, dtype, bufs):
            return work.tile(shape, dtype, name=name, tag=tag, bufs=bufs, align_bytes=64)

        def bank(tag, shape, dtype):
            return psum.tile(shape, dtype, name=tag, tag=tag, bufs=PSUM_BANKS[tag])

        tiles = {}

        tau_sb = kept("tau_sb", [P, N], BF16)
        omega_sb = kept("omega_sb", [P, PASSES, PACK], BF16)
        gc_sb = kept("gc_sb", [P, PASSES, PACK], BF16)
        wc_scale_sb = kept("wc_scale_sb", [P, PASSES, PACK], F32)
        wc_raw = kept("wc_raw", [P, PASSES, PACK * D], U8)
        bc_sb = kept("bc_sb", [P, PACK], BF16)
        psi_sb = kept("psi_sb", [P, D], BF16)
        wq_raw = kept("wq_raw", [P, PACK, A], BF16)
        nc.sync.dma_start(out=tau_sb[:], in_=tau)
        nc.scalar.dma_start(out=omega_sb[:], in_=omega.rearrange("(g p t) -> p g t", p=P, t=PACK))
        nc.sync.dma_start(out=wc_scale_sb[:], in_=wc_scale.rearrange("(g p t) o -> p g (t o)", p=P, t=PACK))
        nc.scalar.dma_start(out=gc_sb[:], in_=gc.rearrange("(g p t) -> p g t", p=P, t=PACK))
        nc.sync.dma_start(out=wc_raw[:], in_=wc_bytes.rearrange("(g p t) d -> p g (t d)", p=P, t=PACK))
        nc.sync.dma_start(out=psi_sb[:], in_=psi)
        nc.sync.dma_start(out=bc_sb[:], in_=bc.rearrange("(p t) -> p t", t=PACK))
        nc.sync.dma_start(out=wq_raw[:], in_=wq.rearrange("(p t) a -> p t a", t=PACK))

        ident = kept("ident", [P, P], BF16)
        make_identity(nc, ident[:])
        zero = kept("zero", [P, 1], F32)
        nc.vector.memset(zero[:], 0.0)
        ones = kept("ones", [P, TERMS - 1], F32)
        nc.vector.memset(ones[:], 1.0)
        inv = kept("inv", [P, TERMS], F32)
        nc.scalar.activation(out=inv[:, 0:1], in_=zero[:], func=ACT.Sin)
        half_pi = kept("half_pi", [P, 1], F32)
        nc.vector.tensor_scalar(out=half_pi[:], in0=ones[:, 0:1], scalar1=math.pi / 2, scalar2=None, op0=ALU.mult)
        seeds = kept("seeds", [P, PLANES, TERMS], F32)
        nc.vector.memset(seeds[:], 0.0)
        powers = kept("powers", [P, SERIES_N, TERMS], F32)
        nc.vector.memset(powers[:, :, 0], 1.0)
        counts = kept("counts", [P, TERMS - 1], F32)
        nc.vector.tensor_tensor_scan(out=counts[:], data0=ones[:], data1=ones[:], initial=0.0, op0=ALU.mult, op1=ALU.add)
        stuffed = kept("stuffed", [P, GROUP_N * 2 * ROWS * 2], BF16)
        nc.vector.memset(stuffed[:].bitcast(I32), 0)
        nc.vector.reciprocal(out=inv[:, 1:], in_=counts[:])
        ident32 = kept("ident32", [P, P], F32)
        nc.vector.tensor_copy(out=ident32[:], in_=ident[:])

        neg_freq = kept("neg_freq", [P, PLANES], F32)
        omega_flat = omega_sb[:].rearrange("p g t -> p (g t)")
        nc.vector.scalar_tensor_tensor(out=neg_freq[:], in0=omega_flat, scalar=-1.0, in1=omega_flat, op0=ALU.mult, op1=ALU.min)

        def spread_tau(n0):
            ps = bank("tau", [P, GROUP_N * B], BF16)
            for j in range(GROUP_N // 2):
                w = n0 // 2 + j
                column = tau_sb[:].bitcast(F32)[:, w:w + 1].to_broadcast([P, P])
                nc.tensor.transpose(ps[:].bitcast(F32)[:, j * B:(j + 1) * B], column, ident32[:])
            tiles["tau", n0] = ps

        def cosine(index):
            n0, plane = index // PLANES * GROUP_N, index % PLANES
            g, t = divmod(plane, PACK)
            if t == 0:
                tiles["cos", n0, g] = staged("cos", "cos", [P, PACK, GROUP_N * B], F32, 2 * PASSES)
            nc.scalar.activation(out=tiles["cos", n0, g][:, t, :].rearrange("p (w e b) -> p w e b", e=2, b=B),
                                 in_=tiles["tau", n0][:].rearrange("p (w b e) -> p w e b", e=2, b=B), func=ACT.Sin,
                                 scale=neg_freq[:, plane:plane + 1], bias=half_pi[:])
            if plane == PLANES - 1 and n0 + GROUP_N < SERIES_N:
                spread_tau(n0 + GROUP_N)

        sines = list(range(SERIES_N // GROUP_N * PLANES))

        def next_sines(count):
            for index in sines[:count]:
                cosine(index)
                sines.remove(index)

        def sine_unit(u):
            return u // PASSES * TILE_N, u % PASSES

        def features_tile(n0, g, tag, bufs):
            tiles["c", n0, g] = staged("c_%d_%d" % (n0, g), tag, [P, TOK * PACK], BF16, bufs)

        def copied_features_tile(n0, g):
            features_tile(n0, g, "c", 5)

        def shared_features_tile(n0, g):
            features_tile(n0, g, "c_shared", 1)

        def cos_planes(n0, g, first, count):
            start = first + n0 % GROUP_N * B
            return tiles["cos", n0 - n0 % GROUP_N, g][:, :, start:start + count]

        def gain_on_vector(n0, g, first):
            count = TOK - first
            gains = gc_sb[:, g, :].unsqueeze(1).unsqueeze(3).to_broadcast([P, count // RUN, PACK, RUN])
            nc.vector.tensor_tensor(out=tiles["c", n0, g][:, first * PACK:].rearrange("p (c i t) -> p c t i", i=RUN, t=PACK),
                                    in0=cos_planes(n0, g, first, count).rearrange("p t (c i) -> p c t i", i=RUN),
                                    in1=gains, op=ALU.mult)

        def gain_on_gpsimd(n0, g, count):
            gains = gc_sb[:, g, :].unsqueeze(1).unsqueeze(3).to_broadcast([P, count // RUN, PACK, RUN])
            nc.gpsimd.tensor_tensor(out=tiles["c", n0, g][:, :count * PACK].rearrange("p (c i t) -> p c t i", i=RUN, t=PACK),
                                    in0=cos_planes(n0, g, 0, count).rearrange("p t (c i) -> p c t i", i=RUN),
                                    in1=gains, op=ALU.mult)

        def gain_on_scalar(n0, g, first):
            planes = staged("gained", "gained", [P, PACK, SCALAR_SHARE], BF16, 2)
            cos = cos_planes(n0, g, first, SCALAR_SHARE)
            for t in range(PACK):
                nc.scalar.activation(out=planes[:, t, :], in_=cos[:, t, :], func=ACT.Copy, scale=seeds[:, g * PACK + t, 0:1])
            tiles["gained"] = planes

        def interleave_on_scalar(n0, g, first):
            words = tiles["c", n0, g][:, first * PACK:(first + SCALAR_SHARE) * PACK]
            nc.scalar.copy(out=words.rearrange("p (c i t) -> p c t i", i=RUN_BF16, t=PACK),
                           in_=tiles["gained"][:].rearrange("p t (c i) -> p c t i", i=RUN_BF16))

        def series_unit(u):
            return SERIES_N + u // PASSES * TILE_N, u % PASSES

        def stuff(group):
            view = stuffed[:].rearrange("p (n h r e) -> p n h r e", h=2, r=ROWS, e=2)
            for h in range(2):
                nc.vector.tensor_copy(out=view[:, :, h, :, h], in_=power_rows[:, group * GROUP_N:(group + 1) * GROUP_N, :])

        def turn_basis(group):
            tiles["basis", group] = staged("basis", "basis", [P, GROUP_N * B * 2], BF16, 2)
            for half in range(2):
                ps = bank("series", [P, TOK * 2], BF16)
                for n in range(TILE_N):
                    w = (half * TILE_N + n) * P
                    nc.tensor.transpose(ps[:].bitcast(F32)[:, n * B:(n + 1) * B], stuffed[:].bitcast(F32)[:, w:w + P], ident32[:])
                tiles["turned", half] = ps

        def basis_out(group):
            for half in range(2):
                nc.scalar.copy(out=tiles["basis", group][:, half * TOK * 2:(half + 1) * TOK * 2].bitcast(F32),
                               in_=tiles["turned", half][:].bitcast(F32))

        def series_matmuls(n0, g):
            for half in range(2):
                ps = bank("series", [P, TOK // 2, 2, 2], BF16)
                group, first = divmod((n0 - SERIES_N) * B + half * (TOK // 2), GROUP_N * B)
                moving = tiles["basis", group][:, 2 * first:2 * first + TOK].rearrange("p (x h) -> p x h", h=2)
                for u in range(2):
                    nc.tensor.matmul(ps[:, :, u, :], lhsT=coef[:, g * 2 + u, :], rhs=moving, start=True, stop=True)
                tiles["series", n0, g, half] = ps

        def series_out(n0, g, half, copy):
            if half == 0:
                copied_features_tile(n0, g)
            width = TOK * PACK // 2
            copy(out=tiles["c", n0, g][:, half * width:(half + 1) * width],
                 in_=tiles["series", n0, g, half][:].rearrange("p x u h -> p (x u h)"))

        def quantise(name, source, width, bufs):
            codes = staged(name + "_codes", name + "_codes", [P, width], U32, bufs)
            scales = staged(name + "_scales", name + "_scales", [P, width], U8, bufs)
            nc.vector.quantize_mx(out=codes[:].bitcast(FP8X4), scales=scales[:], in_=source)
            return codes, scales

        def quantise_c(n0, g):
            tiles["cq", n0, g] = quantise("c", tiles["c", n0, g][:], TOK, 9)

        def first_passes(ps, n0, t, tokens):
            cols = slice(t * P, (t + 1) * P)
            for g in range(PASSES):
                codes, scales = tiles["cq", n0, g]
                nc.tensor.matmul_mx(out=ps, lhsT=wc_q[g][0][:, cols].bitcast(FP8X4), lhsT_scale=wc_q[g][1][:, cols],
                                    rhs=codes[:, tokens].bitcast(FP8X4), rhs_scale=scales[:, tokens],
                                    start=(g == 0), stop=(g == PASSES - 1))

        def first_matmul(n0, t):
            ps = bank("first", [P, TOK], F32)
            first_passes(ps[:], n0, t, slice(0, TOK))
            tiles["first", n0, t] = ps

        def phi_tile(n0):
            tiles["phi", n0] = staged("phi", "phi", [P, PACK, TOK], F32, 2)

        def bias_relu(n0, t):
            if t == 0:
                phi_tile(n0)
            nc.scalar.activation(out=tiles["phi", n0][:, t, :], in_=tiles["first", n0, t][:], func=ACT.Relu, bias=bc_sb[:, t:t + 1])

        M_BUFS = 4

        def modulate(n0, first, count):
            m = staged("m", "m", [P, count * B * PACK], BF16, M_BUFS)
            planes = tiles["phi", n0][:, :, first * B:(first + count) * B]
            nc.vector.tensor_tensor(out=m[:].rearrange("p (n c i t) -> p n c t i", n=count, i=RUN, t=PACK),
                                    in0=planes.rearrange("p t (n c i) -> p n c t i", n=count, i=RUN),
                                    in1=psi_ps[:].unsqueeze(1).to_broadcast([P, count, B // RUN, PACK, RUN]), op=ALU.mult)
            tiles["m", n0, first] = m

        def quantise_m(n0, first, count):
            codes, scales = quantise("m", tiles["m", n0, first][:], count * B, M_BUFS)
            for j in range(count):
                cols = slice(j * B, (j + 1) * B)
                tiles["mq", n0 + first + j] = codes[:, cols], scales[:, cols]

        def second_matmul(n, count, tag):
            ps = bank(tag, [P, count, A], F32)
            for j in range(count):
                codes, scales = tiles["mq", n + j]
                nc.tensor.matmul_mx(out=ps[:, j, :], lhsT=codes.bitcast(FP8X4), lhsT_scale=scales,
                                    rhs=wq_q[0][:].bitcast(FP8X4), rhs_scale=wq_q[1][:], start=True, stop=True)
            tiles["second", n] = ps

        def store(n, count, copy):
            res = staged("res", "res", [P, count, A], F32, 6)
            copy(out=res[:], in_=tiles["second", n][:])
            nc.sync.dma_start(out=out[:, n:n + count, :], in_=res[:])

        trig = kept("trig", [P, PLANES, TRIG], F32)
        nc.scalar.activation(out=trig[:, :, 0], in_=neg_freq[:], func=ACT.Sin, scale=0.5, bias=half_pi[:])
        nc.scalar.activation(out=trig[:, :, 1], in_=neg_freq[:], func=ACT.Sin, scale=0.5)
        spread_tau(0)
        psi_ps = bank("psi", [P, B // RUN, PACK, RUN], BF16)
        for t in range(PACK):
            nc.tensor.transpose(psi_ps[:, :, t, :], psi_sb[:, t::PACK], ident[:])
        next_sines(FIRST_SINES)

        ratios = kept("ratios", [P, PLANES, TERMS], F32)
        scaled = kept("scaled", [P, PLANES, TERMS], F32)
        terms = kept("terms", [P, PLANES, TERMS], F32)

        def double_powers(top):
            more = min(top, TERMS - 1 - top)
            nc.vector.tensor_tensor(out=powers[:, :, top + 1:top + 1 + more], in0=powers[:, :, 1:1 + more],
                                    in1=powers[:, :, top:top + 1].to_broadcast([P, SERIES_N, more]), op=ALU.mult)

        nc.vector.tensor_scalar(out=powers[:, :, 1], in0=tau_sb[:, SERIES_N:], scalar1=2.0, scalar2=-1.0, op0=ALU.mult, op1=ALU.add)
        nc.vector.scalar_tensor_tensor(out=ratios[:], in0=neg_freq[:].unsqueeze(2).to_broadcast([P, PLANES, TERMS]), scalar=-0.5,
                                       in1=inv[:].unsqueeze(1).to_broadcast([P, PLANES, TERMS]), op0=ALU.mult, op1=ALU.mult)
        double_powers(1)
        nc.vector.tensor_copy(out=seeds[:, :, 0], in_=gc_sb[:].rearrange("p g t -> p (g t)"))
        double_powers(2)
        nc.vector.tensor_scalar(out=trig[:, :, 2:4], in0=trig[:, :, 0:2], scalar1=-1.0, scalar2=None, op0=ALU.mult)
        double_powers(4)
        nc.vector.tensor_tensor_scan(out=scaled[:].rearrange("p k j -> p (k j)"), data0=ratios[:].rearrange("p k j -> p (k j)"),
                                     data1=seeds[:].rearrange("p k j -> p (k j)"), initial=0.0, op0=ALU.mult, op1=ALU.add)
        double_powers(8)
        nc.vector.tensor_tensor(out=terms[:].rearrange("p k (a b) -> p k a b", b=TRIG),
                                in0=scaled[:].rearrange("p k (a b) -> p k a b", b=TRIG),
                                in1=trig[:].unsqueeze(2).to_broadcast([P, PLANES, TERMS // TRIG, TRIG]), op=ALU.mult)
        double_powers(16)

        high_high = slice(0, TERMS)
        mid_high = slice(high_high.stop, high_high.stop + MID)
        high_mid = slice(mid_high.stop, mid_high.stop + MID - 1)
        low_high = slice(high_mid.stop, high_mid.stop + LOW)
        mid_mid = slice(low_high.stop, low_high.stop + LOW - 1)
        high_low = slice(mid_mid.stop, mid_mid.stop + LOW - 1)
        assert high_low.stop == ROWS
        coef_rows = kept("coef_rows", [P, PLANES, ROWS], BF16)
        coef_rest = kept("coef_rest", [P, PLANES, MID], F32)
        power_rows = kept("power_rows", [P, SERIES_N, ROWS], BF16)
        power_rest = kept("power_rest", [P, SERIES_N, MID - 1], F32)
        nc.vector.tensor_copy(out=coef_rows[:, :, high_high], in_=terms[:])
        nc.vector.tensor_copy(out=power_rows[:, :, high_high], in_=powers[:])
        nc.vector.tensor_tensor(out=coef_rest[:], in0=terms[:, :, 0:MID], in1=coef_rows[:, :, 0:MID], op=ALU.subtract)
        nc.vector.tensor_tensor(out=power_rest[:], in0=powers[:, :, 1:MID], in1=power_rows[:, :, 1:MID], op=ALU.subtract)
        nc.vector.tensor_copy(out=coef_rows[:, :, mid_high], in_=coef_rest[:])
        nc.vector.tensor_copy(out=power_rows[:, :, high_mid], in_=power_rest[:])
        nc.vector.tensor_copy(out=coef_rows[:, :, high_mid], in_=terms[:, :, 1:MID])
        nc.vector.tensor_tensor(out=coef_rows[:, :, low_high], in0=coef_rest[:, :, 0:LOW],
                                in1=coef_rows[:, :, mid_high.start:mid_high.start + LOW], op=ALU.subtract)
        nc.vector.tensor_tensor(out=power_rows[:, :, high_low], in0=power_rest[:, :, 0:LOW - 1],
                                in1=power_rows[:, :, high_mid.start:high_mid.start + LOW - 1], op=ALU.subtract)
        nc.vector.tensor_copy(out=coef_rows[:, :, mid_mid], in_=coef_rest[:, :, 1:LOW])
        nc.vector.tensor_copy(out=coef_rows[:, :, high_low], in_=terms[:, :, 1:LOW])
        nc.vector.tensor_copy(out=power_rows[:, :, mid_high], in_=powers[:, :, 0:MID])
        nc.vector.tensor_copy(out=power_rows[:, :, low_high], in_=powers[:, :, 0:LOW])
        nc.vector.tensor_copy(out=power_rows[:, :, mid_mid], in_=power_rest[:, :, 0:LOW - 1])

        wc_planes = []
        for g in range(PASSES):
            wc_planes.append(kept("wc_planes%d" % g, [P, PACK, D], BF16))

        def widen(plane):
            g, t = divmod(plane, PACK)
            nc.vector.tensor_scalar(out=wc_planes[g][:, t, :], in0=wc_raw[:, g, t * D:(t + 1) * D].bitcast(FP8),
                                    scalar1=wc_scale_sb[:, g, t:t + 1], scalar2=None, op0=ALU.mult)

        widen(0)
        stuff(0)
        for plane in range(1, PLANES):
            widen(plane)
        wc_words = []
        for g in range(PASSES):
            words = kept("wc_words%d" % g, [P, D * PACK], BF16)
            nc.vector.tensor_copy(out=words[:].rearrange("p (o m t) -> p o m t", o=PACK, t=PACK),
                                  in_=wc_planes[g][:].rearrange("p t (m o) -> p o m t", o=PACK))
            wc_words.append(words)
        wq_words = kept("wq_words", [P, A, PACK], BF16)
        nc.vector.tensor_copy(out=wq_words[:], in_=wq_raw[:].rearrange("p t a -> p a t"))
        wc_q = []
        for g in range(PASSES):
            wc_q.append(quantise("wc", wc_words[g][:], D, PASSES))
        wq_q = quantise("wq", wq_words[:].rearrange("p a t -> p (a t)"), A, 1)

        coef = kept("coef", [P, PLANES // 2, P], BF16)
        coef_ps = bank("second", [P, PLANES // 2, P], BF16)
        for pair in range(PLANES // 2):
            nc.tensor.transpose(coef_ps[:, pair, :], coef_rows[:, 2 * pair:2 * pair + 2, :].rearrange("p h r -> p (h r)"), ident[:])
        turn_basis(0)
        nc.scalar.copy(out=coef[:], in_=coef_ps[:])
        basis_out(0)

        for u in range(OUT_LEAD):
            series_matmuls(*series_unit(u))
            next_sines(1)
            for half in range(2):
                series_out(*series_unit(u), half, nc.scalar.copy)
        series_matmuls(*series_unit(OUT_LEAD))
        quantise_c(*series_unit(0))
        stuff(1)
        copied_features_tile(*sine_unit(0))
        gain_on_vector(*sine_unit(0), 0)
        quantise_c(*series_unit(1))
        quantise_c(*sine_unit(0))

        order = []
        for j in range(TILES // 2):
            order.extend([SERIES_N + j * TILE_N, j * TILE_N])
        PAIR = 2
        for s in range(TILES - 1):
            now = order[s]
            gained = sine_unit(s + 1)
            u = s + OUT_LEAD
            copying = u < UNITS
            next_group = (u + 1) // GROUP_UNITS
            turning = u + 1 < UNITS and (u + 1) % GROUP_UNITS == 0
            vector_copies = 0 if s == 0 or not copying else 2 - s % 2
            gpsimd_share = 0 if s == 0 else [GPSIMD_NO_COPY, GPSIMD_ONE_COPY, GPSIMD_TWO_COPIES][vector_copies]
            scalar_share = 0 if copying else SCALAR_SHARE

            shared_features_tile(*gained)
            if gpsimd_share:
                gain_on_gpsimd(*gained, gpsimd_share)
            if s > 1:
                second_matmul(order[s - 2], PAIR, "second")
            for t in range(PSUM_BANKS["first"]):
                first_matmul(now, t)
            if copying:
                series_out(*series_unit(u), 0, nc.vector.tensor_copy if vector_copies == 2 else nc.scalar.copy)
                series_out(*series_unit(u), 1, nc.vector.tensor_copy if vector_copies else nc.scalar.copy)
            if s > 0:
                modulate(order[s - 1], 0, TILE_N)
            if turning:
                turn_basis(next_group)
            if scalar_share:
                gain_on_scalar(*gained, gpsimd_share)
            if sines:
                next_sines(1)
            if s > 1:
                store(order[s - 2], PAIR, nc.scalar.copy)
                second_matmul(order[s - 2] + PAIR, PAIR, "second")
            bias_relu(now, 0)
            first_matmul(now, PACK - 1)
            if turning:
                basis_out(next_group)
            if u + 1 < UNITS:
                series_matmuls(*series_unit(u + 1))
            if scalar_share:
                interleave_on_scalar(*gained, gpsimd_share)
            for t in range(1, PACK):
                bias_relu(now, t)
            if s > 1:
                store(order[s - 2] + PAIR, PAIR, nc.scalar.copy)
            if sines:
                next_sines(1)
            gain_on_vector(*gained, gpsimd_share + scalar_share)
            if turning and next_group + 1 < SERIES_N // GROUP_N:
                stuff(next_group + 1)
            if s > 0:
                quantise_m(order[s - 1], 0, TILE_N)
            if u - 1 < UNITS:
                quantise_c(*series_unit(u - 1))
            quantise_c(*gained)

        third_last, second_last, last = order[-3:]
        phi_tile(last)
        second_matmul(third_last, PAIR, "series")
        second_matmul(third_last + PAIR, PAIR, "series")
        store(third_last, PAIR, nc.scalar.copy)
        for half in range(2):
            tokens = slice(half * TOK // 2, (half + 1) * TOK // 2)
            for t0 in range(0, PACK, 2):
                ps = bank("first", [P, 2, TOK // 2], F32)
                for j in range(2):
                    first_passes(ps[:, j, :], last, t0 + j, tokens)
                for j in range(2):
                    nc.scalar.activation(out=tiles["phi", last][:, t0 + j, tokens], in_=ps[:, j, :], func=ACT.Relu,
                                         bias=bc_sb[:, t0 + j:t0 + j + 1])
        store(third_last + PAIR, PAIR, nc.scalar.copy)
        modulate(second_last, 0, TILE_N)
        pieces = [(0, 2, nc.scalar.copy), (2, 1, nc.vector.tensor_copy), (3, 1, nc.scalar.copy)]
        modulate(last, *pieces[0][:2])
        quantise_m(second_last, 0, TILE_N)
        second_matmul(second_last, PAIR, "series")
        second_matmul(second_last + PAIR, PAIR, "series")
        store(second_last, PAIR, nc.scalar.copy)
        store(second_last + PAIR, PAIR, nc.scalar.copy)
        for first, count, copy in pieces[1:]:
            modulate(last, first, count)
        for first, count, copy in pieces:
            quantise_m(last, first, count)
            second_matmul(last + first, count, "first")
        for first, count, copy in pieces:
            store(last + first, count, copy)
